import numpy as np
import ml_dtypes


def mxq(x, axis, fmt="e4m3"):
    dtype, down = {"e4m3": (ml_dtypes.float8_e4m3fn, 7), "e5m2": (ml_dtypes.float8_e5m2, 14)}[fmt]
    v = np.moveaxis(np.asarray(x, np.float32).astype(ml_dtypes.bfloat16).astype(np.float64), axis, -1)
    blocks = v.reshape(v.shape[:-1] + (-1, 32))
    amax = np.abs(blocks).max(-1, keepdims=True)
    byte = np.maximum(np.where(amax > 0, np.frexp(amax)[1] - 1 + 127, 0) - down, 1)
    scale = np.exp2(byte - 127.0)
    codes = (blocks / scale).astype(np.float32).astype(dtype).astype(np.float64)
    return np.moveaxis((codes * scale).reshape(v.shape), -1, axis)


WIDE = False


def mx_kscale(k):
    if not WIDE:
        return np.ones(k)
    levels = np.array([10, -10, 5, -5, 0])
    if k % 512:
        return np.exp2(np.random.permutation(np.resize(levels, k // 32))).repeat(32)
    a = np.empty((k // 512, 16))
    for p in range(k // 512):
        a[p, :8] = np.random.permutation(np.resize(levels, 8))
        for g in range(8):
            far = levels[np.abs(levels - a[p, g]) >= 10]
            a[p, g + 8] = far[np.random.randint(len(far))]
    return np.exp2(a.ravel()).repeat(32)


def f64(x):
    return np.asarray(x).astype(np.float64)


def striped(idx):
    return np.tile(idx.reshape(-1, 16).T, (8, 1)).astype(np.uint16)


def unstriped(offs):
    return offs[:16].T.reshape(-1).astype(np.int64)


E2M1 = np.array([0.0, 0.5, 1.0, 1.5, 2.0, 3.0, 4.0, 6.0, -0.0, -0.5, -1.0, -1.5, -2.0, -3.0, -4.0, -6.0])


def pack_weight(w, fmt):
    k, n = w.shape
    w = f64(np.asarray(w, np.float32).astype(ml_dtypes.bfloat16)).reshape(k // 32, 32, n)
    amax = np.abs(w).max(1)
    if fmt == "e4m3":
        byte = np.frexp(amax)[1] - 1 + 127 - 7
    else:
        mant, ex = np.frexp(amax / 6.0)
        byte = np.where(mant > 0.5, ex, ex - 1) + 127
    byte = np.clip(np.where(amax > 0, byte, 1), 1, 254)
    scaled = (w * np.exp2(127.0 - byte)[:, None, :]).reshape(k, n).astype(np.float32)
    by_word = np.ascontiguousarray(scaled.reshape(k // 512, 128, 4, n).transpose(0, 1, 3, 2))
    if fmt == "e4m3":
        words = by_word.astype(ml_dtypes.float8_e4m3fn).view(np.uint8)
    else:
        c = by_word.astype(ml_dtypes.float4_e2m1fn).view(np.uint8) & 0xF
        words = (c[..., 0::2] | (c[..., 1::2] << 4)).reshape(k // 512, 128, 2 * n)
    return np.ascontiguousarray(words), np.ascontiguousarray(byte.astype(np.uint8).reshape(k // 512, 16, n))


def unpack_weight(words, scales, fmt):
    g, _, n = scales.shape
    words = np.ascontiguousarray(words).reshape(g, 128, n, -1)
    if fmt == "e4m3":
        vals = words.view(ml_dtypes.float8_e4m3fn).astype(np.float64)
    else:
        nib = np.empty((g, 128, n, 4), np.uint8)
        nib[..., 0::2] = words & 0xF
        nib[..., 1::2] = words >> 4
        vals = E2M1[nib]
    vals = vals * np.repeat(np.exp2(scales.astype(np.float64) - 127.0), 8, axis=1)[..., None]
    return vals.transpose(0, 1, 3, 2).reshape(g * 512, n)


def gelu(v):
    return 0.5 * v * (1.0 + np.tanh(np.sqrt(2.0 / np.pi) * (v + 0.044715 * v**3)))


K, T, S, H, T3, S2, T2 = 512, 2048, 1024, 1024, 2048, 512, 2048

def setup_inputs():
    n = np.random.standard_normal
    s = mx_kscale(K)[:, None]
    u = mx_kscale(H)[:, None]
    tab_words, tab_scales = pack_weight(n((K, T)) * s, "e4m3")
    tab2_words, tab2_scales = pack_weight(n((H, T3)) / np.sqrt(H) / u, "e4m3")
    w4_words, w4_scales = pack_weight(n((K, H)) / np.sqrt(K) / s, "e2m1")
    w8_words, w8_scales = pack_weight(n((K, S2)) / np.sqrt(K) / s, "e4m3")
    return {
        "tab_words": tab_words, "tab_scales": tab_scales,
        "tab2_words": tab2_words, "tab2_scales": tab2_scales,
        "w1": (n((K, H)) / np.sqrt(K) / s).astype(np.float32),
        "w4_words": w4_words, "w4_scales": w4_scales,
        "w8_words": w8_words, "w8_scales": w8_scales,
        "gain": (np.random.uniform(0.5, 1.0, H) * u[:, 0]).astype(np.float32),
        "prior": (0.7 * n(S2)).astype(np.float32),
        "field": (0.7 * n((S2, S))).astype(np.float32),
        "page1": n((S2, T2)).astype(np.float32),
        "wgo": np.exp(0.3 * n((128, S))).astype(np.float32),
        "offs": striped(np.random.permutation(T)[:S]),
        "offs2": striped(np.random.permutation(T3)[:S2]),
        "offs3": striped(np.random.permutation(T2)[:S]),
    }

def reference(tab_words, tab_scales, tab2_words, tab2_scales, w1, w4_words, w4_scales,
              w8_words, w8_scales, gain, prior, field, page1, wgo, offs, offs2, offs3):
    v = unpack_weight(tab_words, tab_scales, "e4m3")[:, unstriped(offs)]
    v2 = unpack_weight(tab2_words, tab2_scales, "e4m3")[:, unstriped(offs2)]
    w4 = unpack_weight(w4_words, w4_scales, "e2m1")
    w8 = unpack_weight(w8_words, w8_scales, "e4m3")
    a = mxq(f64(w1), 0, "e4m3").T @ v
    b = w4.T @ v
    h = f64(gain)[:, None] * (a + np.tanh(a + b))
    e = v2.T @ mxq(h, 0, "e4m3")
    d = w8.T @ v
    y = np.maximum(e + f64(prior)[:, None], d + f64(field))
    out = f64(page1).copy()
    out[:, unstriped(offs3)] = np.tile(f64(wgo), (S2 // 128, 1)) * y
    return out

@@ -1,0 +1,310 @@
+from contextlib import ExitStack
+
+import concourse.mybir as mybir
+from concourse.masks import make_identity
+
+K, T, S, H, T3, S2, T2 = 512, 2048, 1024, 1024, 2048, 512, 2048
+FLOPS = 2 * S * (2 * K * H + H * S2 + K * S2)
+
+F32 = mybir.dt.float32
+BF16 = mybir.dt.bfloat16
+I32 = mybir.dt.int32
+U32 = mybir.dt.uint32
+U16 = mybir.dt.uint16
+U8 = mybir.dt.uint8
+FP8X4 = mybir.dt.float8_e4m3fn_x4
+FP4X4 = mybir.dt.float4_e2m1fn_x4
+ALU = mybir.AluOpType
+ACT = mybir.ActivationFunctionType
+
+P = 128
+NB = 512
+CH = 256
+NCH = S // CH
+GW = 512
+NG = S // GW
+JT = CH // P
+ON_SCALAR = ((0, 0), (0, 1), (1, 0), (1, 1), (2, 0), (2, 1), (3, 0), (3, 1),)
+
+
+def tile_list_bridge_board_comparison_kernel(
+    tc, tab_words, tab_scales, tab2_words, tab2_scales, w1, w4_words, w4_scales,
+    w8_words, w8_scales, gain, prior, field, page1, wgo, offs, offs2, offs3, out,
+):
+    nc = tc.nc
+    with ExitStack() as ctx:
+        keep = ctx.enter_context(tc.tile_pool(name="keep", bufs=1))
+        work = ctx.enter_context(tc.tile_pool(name="work", bufs=3))
+        psum = ctx.enter_context(tc.psum_pool(name="psum", bufs=2))
+
+        def held(shape, dtype, name):
+            return keep.tile(shape, dtype, name=name, align_bytes=64)
+
+        idx = held([P, S // 16], U16, "idx")
+        idx2 = held([P, S2 // 16], U16, "idx2")
+        idx3 = held([P, S // 16], U16, "idx3")
+        tabw = held([P, T], U32, "tabw")
+        tabs = held([P, T], U8, "tabs")
+        tab2w = [held([P, T3], U32, "tab2w%d" % a) for a in range(2)]
+        tab2s = held([P, T3], U8, "tab2s")
+        w1raw = [held([P, 4, NB // 2], F32, "w1raw%d" % a) for a in range(4)]
+        w1b = [held([P, NB, 4], BF16, "w1b%d" % a) for a in range(2)]
+        w1q = [held([P, NB], U32, "w1q%d" % a) for a in range(2)]
+        w1s = [held([P, NB], U8, "w1s%d" % a) for a in range(2)]
+        w4w = held([P, 2 * H], U8, "w4w")
+        w4s = held([P, H], U8, "w4s")
+        w8w = held([P, S2], U32, "w8w")
+        w8s = held([P, S2], U8, "w8s")
+        g = held([P, 2, 4], F32, "g")
+        pri = held([P, 4], F32, "pri")
+        fld = [[held([P, GW], F32, "fld%d_%d" % (gc, m)) for m in range(4)] for gc in range(NG)]
+        page = [held([P, T2], F32, "page%d" % m) for m in range(4)]
+        wg = [held([P, GW], F32, "wg%d" % gc) for gc in range(NG)]
+        ident = held([P, P], F32, "ident")
+        vw = [held([P, GW], U32, "vw%d" % c) for c in range(NG)]
+        vs = [held([P, GW], U8, "vs%d" % c) for c in range(NG)]
+        v2w = [held([P, S2], U32, "v2w%d" % a) for a in range(2)]
+        v2s = held([P, S2], U8, "v2s")
+        hq = [[held([P, CH], U32, "hq%d_%d" % (c, a)) for a in range(2)] for c in range(NCH)]
+        hs = [[held([P, CH], U8, "hs%d_%d" % (c, a)) for a in range(2)] for c in range(NCH)]
+
+        for plane in (w4s, tab2s, w8s):
+            nc.vector.memset(plane[:].bitcast(I32), 0)
+        make_identity(nc, ident[:])
+
+        def load_rows(plane, dram, q):
+            passes = dram.shape[0]
+            nc.sync.dma_start(
+                out=plane[32 * q : 32 * q + 4 * passes, :].bitcast(I32),
+                in_=dram[:, 4 * q : 4 * q + 4, :].bitcast(I32),
+            )
+
+        def load_tab_rows(q):
+            nc.sync.dma_start(
+                out=tabs[32 * q : 32 * q + 32, :].bitcast(I32),
+                in_=tab_scales[:, 4 * q : 4 * q + 4, :].bitcast(I32).to_broadcast([8, 4, T // 4]),
+            )
+
+        def load_words(tile, dram):
+            nc.sync.dma_start(out=tile[:].bitcast(I32), in_=dram.rearrange("p t i -> p (t i)").bitcast(I32))
+
+        w1v = w1.rearrange("(p i) r -> p i r", i=4)
+
+        def load_w1(q):
+            nc.sync.dma_start(out=w1raw[q][:], in_=w1v[:, :, q * NB // 2 : (q + 1) * NB // 2])
+
+        def load_field(gc, m):
+            nc.sync.dma_start(out=fld[gc][m][:], in_=field[m * P : (m + 1) * P, gc * GW : (gc + 1) * GW])
+
+        def load_page(m):
+            nc.sync.dma_start(out=page[m][:], in_=page1[m * P : (m + 1) * P, :])
+
+        def load_wg(gc):
+            nc.sync.dma_start(out=wg[gc][:], in_=wgo[:, gc * GW : (gc + 1) * GW])
+
+        def load_prior():
+            with nc.allow_non_contiguous_dma(reason="one value of prior to a partition"):
+                nc.sync.dma_start(out=pri[:], in_=prior.rearrange("(m p) -> p m", p=P))
+
+        def load_gain():
+            nc.sync.dma_start(out=g[:], in_=gain.rearrange("(a p t) -> p a t", a=2, t=4))
+
+        def load_w4():
+            nc.sync.dma_start(out=w4w[:].bitcast(I32), in_=w4_words[0].bitcast(I32))
+
+        nc.sync.dma_start(idx[:], offs)
+        load_tab_rows(0)
+        load_tab_rows(1)
+        load_tab_rows(2)
+        load_tab_rows(3)
+        load_w1(0)
+        load_words(tabw, tab_words[0])
+        load_w1(1)
+        load_w4()
+        load_rows(w4s, w4_scales, 0)
+        load_rows(w4s, w4_scales, 1)
+        load_rows(w4s, w4_scales, 2)
+        load_rows(w4s, w4_scales, 3)
+        load_w1(2)
+        load_w1(3)
+        load_gain()
+        nc.sync.dma_start(idx2[:], offs2)
+        load_words(tab2w[0], tab2_words[0])
+        load_rows(tab2s, tab2_scales, 0)
+        load_rows(tab2s, tab2_scales, 1)
+        load_words(tab2w[1], tab2_words[1])
+        load_rows(tab2s, tab2_scales, 2)
+        load_rows(tab2s, tab2_scales, 3)
+        load_words(w8w, w8_words[0])
+        load_rows(w8s, w8_scales, 0)
+        load_rows(w8s, w8_scales, 1)
+        load_field(0, 0)
+        load_rows(w8s, w8_scales, 2)
+        load_rows(w8s, w8_scales, 3)
+        load_wg(0)
+        load_page(0)
+        nc.sync.dma_start(idx3[:], offs3)
+        load_prior()
+        load_field(0, 1)
+        load_page(1)
+        load_field(0, 2)
+        load_page(2)
+        load_field(0, 3)
+        load_page(3)
+        load_wg(1)
+        load_field(1, 0)
+        load_field(1, 1)
+        load_field(1, 2)
+        load_field(1, 3)
+
+        def gather_vs(c):
+            nc.vector.tensor_copy(out=vs[c][:], in_=tabs[:].indirect(idx[:, c * GW // 16 : (c + 1) * GW // 16]))
+
+        def gather_vw(c):
+            nc.vector.tensor_copy(out=vw[c][:], in_=tabw[:].indirect(idx[:, c * GW // 16 : (c + 1) * GW // 16]))
+
+        def gather_v2w(a):
+            nc.vector.tensor_copy(out=v2w[a][:], in_=tab2w[a][:].indirect(idx2[:]))
+
+        def gather_v2s():
+            nc.vector.tensor_copy(out=v2s[:], in_=tab2s[:].indirect(idx2[:]))
+
+        def cast_w1(q, eng):
+            dst = w1b[q // 2][:, q % 2 * NB // 2 : (q % 2 + 1) * NB // 2, :]
+            src = w1raw[q][:].rearrange("p i r -> p r i")
+            if eng == "s":
+                nc.scalar.copy(out=dst, in_=src)
+            elif eng == "v":
+                nc.vector.tensor_copy(out=dst, in_=src)
+            else:
+                nc.gpsimd.tensor_scalar(out=dst, in0=src, scalar1=1.0, scalar2=0.0, op0=ALU.mult, op1=ALU.add)
+
+        def quant_w1(a):
+            nc.vector.quantize_mx(out=w1q[a][:].bitcast(FP8X4), scales=w1s[a][:], in_=w1b[a][:].rearrange("p r i -> p (r i)"))
+
+        def deals(c, lo, n):
+            j0 = c * CH + lo
+            cols = slice(j0 % GW, j0 % GW + n)
+            return vw[j0 // GW][:, cols].bitcast(FP8X4), vs[j0 // GW][:, cols]
+
+        AT, sT, tT, hb = {}, {}, {}, {}
+
+        def first(c, a, jl):
+            w, sc = deals(c, jl * P, P)
+            aT = psum.tile([P, NB], F32, name="aT", bufs=2)
+            nc.tensor.matmul_mx(out=aT[:], lhsT=w, lhsT_scale=sc, rhs=w1q[a][:].bitcast(FP8X4), rhs_scale=w1s[a][:], start=True, stop=True)
+            AT[c, a, jl] = work.tile([P, 4, P], F32, name="AT", bufs=12)
+            nc.scalar.copy(out=AT[c, a, jl][:], in_=aT[:].rearrange("j (p t) -> j t p", t=4))
+
+        def second(c, a, jl):
+            w, sc = deals(c, jl * P, P)
+            bT = psum.tile([P, NB], F32, name="bT", bufs=2)
+            nc.tensor.matmul_mx(out=bT[:], lhsT=w, lhsT_scale=sc, rhs=w4w[:, 2 * NB * a : 2 * NB * (a + 1)].bitcast(FP4X4),
+                                rhs_scale=w4s[:, NB * a : NB * (a + 1)], start=True, stop=True)
+            sT[c, a, jl] = work.tile([P, 4, P], F32, name="sT", bufs=8)
+            nc.vector.tensor_tensor(out=sT[c, a, jl][:], in0=bT[:].rearrange("j (p t) -> j t p", t=4), in1=AT[c, a, jl][:], op=ALU.add)
+
+        def squash(c, a, jl):
+            tT[c, a, jl] = work.tile([P, 4, P], F32, name="tT", bufs=4)
+            nc.scalar.activation(out=tT[c, a, jl][:], in_=sT[c, a, jl][:], func=ACT.Tanh)
+
+        def turn(dst, c, a, jl, t):
+            nc.tensor.matmul(dst, lhsT=AT[c, a, jl][:, t, :], rhs=ident[:], is_transpose=True, start=True, stop=False)
+            nc.tensor.matmul(dst, lhsT=tT[c, a, jl][:, t, :], rhs=ident[:], is_transpose=True, start=False, stop=True)
+
+        def finish(c, a):
+            hb[c, a] = work.tile([P, CH, 4], BF16, name="hb", align_bytes=64)
+            if (c, a) in ON_SCALAR:
+                flat = work.tile([P, 4, CH], BF16, name="flat", bufs=2)
+                for half in range(2):
+                    U = psum.tile([P, 2, CH], F32, name="U", tag="U", bufs=2)
+                    for t in range(2):
+                        for jl in range(JT):
+                            turn(U[:, t, jl * P : (jl + 1) * P], c, a, jl, 2 * half + t)
+                    for t in range(2):
+                        nc.scalar.activation(out=flat[:, 2 * half + t, :], in_=U[:, t, :], func=ACT.Copy,
+                                             scale=g[:, a, 2 * half + t : 2 * half + t + 1])
+                nc.scalar.copy(out=hb[c, a][:], in_=flat[:].rearrange("p t n -> p n t"))
+            else:
+                for jl in range(JT):
+                    U = psum.tile([P, 4, P], F32, name="U", tag="U", bufs=2)
+                    for t in range(4):
+                        turn(U[:, t, :], c, a, jl, t)
+                    nc.vector.tensor_tensor(out=hb[c, a][:, jl * P : (jl + 1) * P, :], in0=U[:].rearrange("p t n -> p n t"),
+                                            in1=g[:, a, :].unsqueeze(1).to_broadcast([P, P, 4]), op=ALU.mult)
+
+        def quant_h(c, a):
+            nc.vector.quantize_mx(out=hq[c][a][:].bitcast(FP8X4), scales=hs[c][a][:], in_=hb[c, a][:].rearrange("p n t -> p (n t)"))
+
+        ys, dfs = {}, {}
+
+        def score_d(gc, m):
+            mc = slice(m * P, (m + 1) * P)
+            d = psum.tile([P, GW], F32, name="d", tag="ed", bufs=2)
+            nc.tensor.matmul_mx(out=d[:], lhsT=w8w[:, mc].bitcast(FP8X4), lhsT_scale=w8s[:, mc],
+                                rhs=vw[gc][:].bitcast(FP8X4), rhs_scale=vs[gc][:], start=True, stop=True)
+            df = work.tile([P, GW], F32, name="df", bufs=8)
+            nc.vector.tensor_tensor(out=df[:], in0=d[:], in1=fld[gc][m][:], op=ALU.add)
+            dfs[gc, m] = df
+
+        def score_e(c, m):
+            mc = slice(m * P, (m + 1) * P)
+            e = psum.tile([P, CH], F32, name="e", tag="ed", bufs=2)
+            for a in range(2):
+                nc.tensor.matmul_mx(out=e[:], lhsT=v2w[a][:, mc].bitcast(FP8X4), lhsT_scale=v2s[4 * a : P, mc],
+                                    rhs=hq[c][a][:].bitcast(FP8X4), rhs_scale=hs[c][a][:], start=(a == 0), stop=(a == 1))
+            y = work.tile([P, CH], F32, name="y", bufs=4)
+            gc, lo = divmod(c * CH, GW)
+            nc.vector.scalar_tensor_tensor(out=y[:], in0=e[:], scalar=pri[:, m : m + 1], in1=dfs[gc, m][:, lo : lo + CH], op0=ALU.add, op1=ALU.max)
+            ys[c, m] = y
+
+        def put(c, m):
+            o = idx3[:, c * CH // 16 : (c + 1) * CH // 16]
+            gc, lo = divmod(c * CH, GW)
+            nc.vector.tensor_tensor(out=page[m][:].indirect(o), in0=ys[c, m][:], in1=wg[gc][:, lo : lo + CH], op=ALU.mult)
+            if c == NCH - 1:
+                nc.sync.dma_start(out=out[m * P : (m + 1) * P, :], in_=page[m][:])
+
+        units = [(a, jl) for a in range(2) for jl in range(JT)]
+
+        gather_vs(0)
+        gather_vs(1)
+        gather_vw(0)
+        cast_w1(0, "s")
+        cast_w1(1, "s")
+        gather_vw(1)
+        quant_w1(0)
+        cast_w1(2, "s")
+        cast_w1(3, "v")
+        for c in range(2):
+            for jl in range(JT):
+                first(c, 0, jl)
+                second(c, 0, jl)
+        quant_w1(1)
+        for jl in range(JT):
+            first(0, 1, jl)
+            second(0, 1, jl)
+        for a, jl in units:
+            squash(0, a, jl)
+        gather_v2w(0)
+        gather_v2w(1)
+        gather_v2s()
+        for jl in range(JT):
+            first(1, 1, jl)
+            second(1, 1, jl)
+        for c in range(NCH):
+            for a in range(2):
+                finish(c, a)
+                quant_h(c, a)
+            if c + 2 < NCH:
+                for a, jl in units:
+                    first(c + 2, a, jl)
+                    second(c + 2, a, jl)
+            for m in range(4):
+                if c % 2 == 0:
+                    score_d(c // 2, m)
+                score_e(c, m)
+                put(c, m)
+            if c + 1 < NCH:
+                for a, jl in units:
+                    squash(c + 1, a, jl)

@@ -35,7 +35,7 @@ def tile_list_bridge_board_comparison_kernel(
     with ExitStack() as ctx:
         keep = ctx.enter_context(tc.tile_pool(name="keep", bufs=1))
         work = ctx.enter_context(tc.tile_pool(name="work", bufs=3))
-        psum = ctx.enter_context(tc.psum_pool(name="psum", bufs=2))
+        psum = ctx.enter_context(tc.psum_pool(name="psum", bufs=1))
 
         def held(shape, dtype, name):
             return keep.tile(shape, dtype, name=name, align_bytes=64)
@@ -65,8 +65,9 @@ def tile_list_bridge_board_comparison_kernel(
         vs = [held([P, GW], U8, "vs%d" % c) for c in range(NG)]
         v2w = [held([P, S2], U32, "v2w%d" % a) for a in range(2)]
         v2s = held([P, S2], U8, "v2s")
-        hq = [[held([P, CH], U32, "hq%d_%d" % (c, a)) for a in range(2)] for c in range(NCH)]
-        hs = [[held([P, CH], U8, "hs%d_%d" % (c, a)) for a in range(2)] for c in range(NCH)]
+        hb = [held([P, 2, CH, 4], BF16, "hb%d" % c) for c in range(NCH)]
+        hq = [held([P, 2, CH], U32, "hq%d" % c) for c in range(NCH)]
+        hs = [held([P, 2, CH], U8, "hs%d" % c) for c in range(NCH)]
 
         for plane in (w4s, tab2s, w8s):
             nc.vector.memset(plane[:].bitcast(I32), 0)
@@ -117,8 +118,8 @@ def tile_list_bridge_board_comparison_kernel(
         load_tab_rows(1)
         load_tab_rows(2)
         load_tab_rows(3)
-        load_w1(0)
         load_words(tabw, tab_words[0])
+        load_w1(0)
         load_w1(1)
         load_w4()
         load_rows(w4s, w4_scales, 0)
@@ -141,21 +142,21 @@ def tile_list_bridge_board_comparison_kernel(
         load_field(0, 0)
         load_rows(w8s, w8_scales, 2)
         load_rows(w8s, w8_scales, 3)
-        load_wg(0)
-        load_page(0)
-        nc.sync.dma_start(idx3[:], offs3)
-        load_prior()
         load_field(0, 1)
-        load_page(1)
         load_field(0, 2)
-        load_page(2)
         load_field(0, 3)
-        load_page(3)
-        load_wg(1)
+        nc.sync.dma_start(idx3[:], offs3)
         load_field(1, 0)
+        load_prior()
         load_field(1, 1)
         load_field(1, 2)
         load_field(1, 3)
+        load_wg(0)
+        load_page(0)
+        load_page(1)
+        load_page(2)
+        load_page(3)
+        load_wg(1)
 
         def gather_vs(c):
             nc.vector.tensor_copy(out=vs[c][:], in_=tabs[:].indirect(idx[:, c * GW // 16 : (c + 1) * GW // 16]))
@@ -187,76 +188,93 @@ def tile_list_bridge_board_comparison_kernel(
             cols = slice(j0 % GW, j0 % GW + n)
             return vw[j0 // GW][:, cols].bitcast(FP8X4), vs[j0 // GW][:, cols]
 
-        AT, sT, tT, hb = {}, {}, {}, {}
+        def ring(name, n):
+            return [psum.tile([P, NB], F32, name="%s%d" % (name, i)) for i in range(n)]
+
+        def take(banks):
+            banks.append(banks.pop(0))
+            return banks[-1][:]
+
+        ring_a, ring_u, ring_v = ring("bank_a", 2), ring("bank_u", 2), ring("bank_v", 4)
+        AT, sT, tT = {}, {}, {}
 
         def first(c, a, jl):
             w, sc = deals(c, jl * P, P)
-            aT = psum.tile([P, NB], F32, name="aT", bufs=2)
+            aT = take(ring_a)
             nc.tensor.matmul_mx(out=aT[:], lhsT=w, lhsT_scale=sc, rhs=w1q[a][:].bitcast(FP8X4), rhs_scale=w1s[a][:], start=True, stop=True)
-            AT[c, a, jl] = work.tile([P, 4, P], F32, name="AT", bufs=12)
-            nc.scalar.copy(out=AT[c, a, jl][:], in_=aT[:].rearrange("j (p t) -> j t p", t=4))
+            AT[c, a, jl] = work.tile([P, 2, P, 2], F32, name="AT", bufs=12)
+            nc.scalar.copy(out=AT[c, a, jl][:], in_=aT[:].rearrange("j (p u e) -> j u p e", u=2, e=2))
 
         def second(c, a, jl):
             w, sc = deals(c, jl * P, P)
-            bT = psum.tile([P, NB], F32, name="bT", bufs=2)
+            bT = take(ring_v)
             nc.tensor.matmul_mx(out=bT[:], lhsT=w, lhsT_scale=sc, rhs=w4w[:, 2 * NB * a : 2 * NB * (a + 1)].bitcast(FP4X4),
                                 rhs_scale=w4s[:, NB * a : NB * (a + 1)], start=True, stop=True)
-            sT[c, a, jl] = work.tile([P, 4, P], F32, name="sT", bufs=8)
-            nc.vector.tensor_tensor(out=sT[c, a, jl][:], in0=bT[:].rearrange("j (p t) -> j t p", t=4), in1=AT[c, a, jl][:], op=ALU.add)
+            sT[c, a, jl] = work.tile([P, 2, P, 2], F32, name="sT", bufs=8)
+            nc.vector.tensor_tensor(out=sT[c, a, jl][:], in0=bT[:].rearrange("j (p u e) -> j u p e", u=2, e=2), in1=AT[c, a, jl][:], op=ALU.add)
 
         def squash(c, a, jl):
-            tT[c, a, jl] = work.tile([P, 4, P], F32, name="tT", bufs=4)
+            tT[c, a, jl] = work.tile([P, 2, P, 2], F32, name="tT", bufs=4)
             nc.scalar.activation(out=tT[c, a, jl][:], in_=sT[c, a, jl][:], func=ACT.Tanh)
 
         def turn(dst, c, a, jl, t):
-            nc.tensor.matmul(dst, lhsT=AT[c, a, jl][:, t, :], rhs=ident[:], is_transpose=True, start=True, stop=False)
-            nc.tensor.matmul(dst, lhsT=tT[c, a, jl][:, t, :], rhs=ident[:], is_transpose=True, start=False, stop=True)
+            nc.tensor.matmul(dst, lhsT=AT[c, a, jl][:, t // 2, :, t % 2], rhs=ident[:], is_transpose=True, start=True, stop=False)
+            nc.tensor.matmul(dst, lhsT=tT[c, a, jl][:, t // 2, :, t % 2], rhs=ident[:], is_transpose=True, start=False, stop=True)
 
         def finish(c, a):
-            hb[c, a] = work.tile([P, CH, 4], BF16, name="hb", align_bytes=64)
             if (c, a) in ON_SCALAR:
                 flat = work.tile([P, 4, CH], BF16, name="flat", bufs=2)
                 for half in range(2):
-                    U = psum.tile([P, 2, CH], F32, name="U", tag="U", bufs=2)
+                    U = take(ring_u).rearrange("p (t n) -> p t n", t=2)
                     for t in range(2):
                         for jl in range(JT):
                             turn(U[:, t, jl * P : (jl + 1) * P], c, a, jl, 2 * half + t)
                     for t in range(2):
                         nc.scalar.activation(out=flat[:, 2 * half + t, :], in_=U[:, t, :], func=ACT.Copy,
                                              scale=g[:, a, 2 * half + t : 2 * half + t + 1])
-                nc.scalar.copy(out=hb[c, a][:], in_=flat[:].rearrange("p t n -> p n t"))
+                nc.scalar.copy(out=hb[c][:, a], in_=flat[:].rearrange("p t n -> p n t"))
             else:
                 for jl in range(JT):
-                    U = psum.tile([P, 4, P], F32, name="U", tag="U", bufs=2)
+                    U = take(ring_u).rearrange("p (t n) -> p t n", t=4)
                     for t in range(4):
                         turn(U[:, t, :], c, a, jl, t)
-                    nc.vector.tensor_tensor(out=hb[c, a][:, jl * P : (jl + 1) * P, :], in0=U[:].rearrange("p t n -> p n t"),
+                    nc.vector.tensor_tensor(out=hb[c][:, a, jl * P : (jl + 1) * P, :], in0=U[:].rearrange("p t n -> p n t"),
                                             in1=g[:, a, :].unsqueeze(1).to_broadcast([P, P, 4]), op=ALU.mult)
 
-        def quant_h(c, a):
-            nc.vector.quantize_mx(out=hq[c][a][:].bitcast(FP8X4), scales=hs[c][a][:], in_=hb[c, a][:].rearrange("p n t -> p (n t)"))
+        def quant_h(c):
+            nc.vector.quantize_mx(out=hq[c][:].rearrange("p a n -> p (a n)").bitcast(FP8X4), scales=hs[c][:].rearrange("p a n -> p (a n)"),
+                                  in_=hb[c][:].rearrange("p a n t -> p (a n t)"))
 
-        ys, dfs = {}, {}
+        ys, dfs, es = {}, {}, {}
 
         def score_d(gc, m):
             mc = slice(m * P, (m + 1) * P)
-            d = psum.tile([P, GW], F32, name="d", tag="ed", bufs=2)
+            d = take(ring_v)
             nc.tensor.matmul_mx(out=d[:], lhsT=w8w[:, mc].bitcast(FP8X4), lhsT_scale=w8s[:, mc],
                                 rhs=vw[gc][:].bitcast(FP8X4), rhs_scale=vs[gc][:], start=True, stop=True)
             df = work.tile([P, GW], F32, name="df", bufs=8)
             nc.vector.tensor_tensor(out=df[:], in0=d[:], in1=fld[gc][m][:], op=ALU.add)
             dfs[gc, m] = df
 
-        def score_e(c, m):
-            mc = slice(m * P, (m + 1) * P)
-            e = psum.tile([P, CH], F32, name="e", tag="ed", bufs=2)
-            for a in range(2):
-                nc.tensor.matmul_mx(out=e[:], lhsT=v2w[a][:, mc].bitcast(FP8X4), lhsT_scale=v2s[4 * a : P, mc],
-                                    rhs=hq[c][a][:].bitcast(FP8X4), rhs_scale=hs[c][a][:], start=(a == 0), stop=(a == 1))
-            y = work.tile([P, CH], F32, name="y", bufs=4)
+        def score_e(c, pair):
+            e = take(ring_v).rearrange("p (i n) -> p i n", i=2)
+            for i in range(2):
+                mc = slice((2 * pair + i) * P, (2 * pair + i + 1) * P)
+                for a in range(2):
+                    nc.tensor.matmul_mx(out=e[:, i, :], lhsT=v2w[a][:, mc].bitcast(FP8X4), lhsT_scale=v2s[4 * a : P, mc],
+                                        rhs=hq[c][:, a, :].bitcast(FP8X4), rhs_scale=hs[c][:, a, :], start=(a == 0), stop=(a == 1))
+            es[c, pair] = e
+
+        def keep_larger(c, pair):
+            e = es[c, pair]
             gc, lo = divmod(c * CH, GW)
-            nc.vector.scalar_tensor_tensor(out=y[:], in0=e[:], scalar=pri[:, m : m + 1], in1=dfs[gc, m][:, lo : lo + CH], op0=ALU.add, op1=ALU.max)
-            ys[c, m] = y
+            for i in range(2):
+                m = 2 * pair + i
+                if pair == 1 and c + 1 < NCH:
+                    ys[c, m] = hb[c + 1][:].rearrange("p a n t -> p (a n t)").bitcast(F32)[:, i * CH : (i + 1) * CH]
+                else:
+                    ys[c, m] = work.tile([P, CH], F32, name="y", bufs=4)
+                nc.vector.scalar_tensor_tensor(out=ys[c, m][:], in0=e[:, i, :], scalar=pri[:, m : m + 1], in1=dfs[gc, m][:, lo : lo + CH], op0=ALU.add, op1=ALU.max)
 
         def put(c, m):
             o = idx3[:, c * CH // 16 : (c + 1) * CH // 16]
@@ -271,40 +289,49 @@ def tile_list_bridge_board_comparison_kernel(
         gather_vs(1)
         gather_vw(0)
         cast_w1(0, "s")
-        cast_w1(1, "s")
         gather_vw(1)
+        cast_w1(1, "s")
         quant_w1(0)
+        for jl in range(JT):
+            first(0, 0, jl)
+            second(0, 0, jl)
         cast_w1(2, "s")
         cast_w1(3, "v")
+        for jl in range(JT):
+            first(1, 0, jl)
+            second(1, 0, jl)
+        quant_w1(1)
         for c in range(2):
             for jl in range(JT):
-                first(c, 0, jl)
-                second(c, 0, jl)
-        quant_w1(1)
-        for jl in range(JT):
-            first(0, 1, jl)
-            second(0, 1, jl)
-        for a, jl in units:
-            squash(0, a, jl)
+                first(c, 1, jl)
+                second(c, 1, jl)
         gather_v2w(0)
         gather_v2w(1)
         gather_v2s()
-        for jl in range(JT):
-            first(1, 1, jl)
-            second(1, 1, jl)
+        D_AT = {0: [(0, 0), (0, 1), (0, 2), (0, 3)], 1: [(1, 0), (1, 1), (1, 2), (1, 3)]}
         for c in range(NCH):
             for a in range(2):
+                for jl in range(JT):
+                    squash(c, a, jl)
+            for a in range(2):
                 finish(c, a)
-                quant_h(c, a)
+            quant_h(c)
+            if c > 0:
+                keep_larger(c - 1, 1)
             if c + 2 < NCH:
                 for a, jl in units:
                     first(c + 2, a, jl)
                     second(c + 2, a, jl)
-            for m in range(4):
-                if c % 2 == 0:
-                    score_d(c // 2, m)
-                score_e(c, m)
-                put(c, m)
-            if c + 1 < NCH:
-                for a, jl in units:
-                    squash(c + 1, a, jl)
+            for gc, m in D_AT.get(c, []):
+                score_d(gc, m)
+            score_e(c, 0)
+            score_e(c, 1)
+            if c > 0:
+                put(c - 1, 2)
+                put(c - 1, 3)
+            keep_larger(c, 0)
+            put(c, 0)
+            put(c, 1)
+        keep_larger(NCH - 1, 1)
+        put(NCH - 1, 2)
+        put(NCH - 1, 3)

@@ -24,7 +24,8 @@ NCH = S // CH
 GW = 512
 NG = S // GW
 JT = CH // P
-ON_SCALAR = ((0, 0), (0, 1), (1, 0), (1, 1), (2, 0), (2, 1), (3, 0), (3, 1),)
+LATE = 2
+ON_SCALAR = ((0, 0), (1, 0), (1, 1), (2, 0), (2, 1), (3, 0), (3, 1))
 
 
 def tile_list_bridge_board_comparison_kernel(
@@ -48,18 +49,20 @@ def tile_list_bridge_board_comparison_kernel(
         tab2w = [held([P, T3], U32, "tab2w%d" % a) for a in range(2)]
         tab2s = held([P, T3], U8, "tab2s")
         w1raw = [held([P, 4, NB // 2], F32, "w1raw%d" % a) for a in range(4)]
-        w1b = [held([P, NB, 4], BF16, "w1b%d" % a) for a in range(2)]
+        w1b = [held([P, NB, 4], BF16, "w1b")] * 2
         w1q = [held([P, NB], U32, "w1q%d" % a) for a in range(2)]
         w1s = [held([P, NB], U8, "w1s%d" % a) for a in range(2)]
         w4w = held([P, 2 * H], U8, "w4w")
         w4s = held([P, H], U8, "w4s")
+        w4w_d = held([P, 2 * H], U8, "w4w_d")
+        w4s_d = held([P, H], U8, "w4s_d")
         w8w = held([P, S2], U32, "w8w")
         w8s = held([P, S2], U8, "w8s")
         g = held([P, 2, 4], F32, "g")
         pri = held([P, 4], F32, "pri")
-        fld = [[held([P, GW], F32, "fld%d_%d" % (gc, m)) for m in range(4)] for gc in range(NG)]
+        fld = [held([P, S], F32, "fld%d" % m) for m in range(4)]
         page = [held([P, T2], F32, "page%d" % m) for m in range(4)]
-        wg = [held([P, GW], F32, "wg%d" % gc) for gc in range(NG)]
+        wg = held([P, S], F32, "wg")
         ident = held([P, P], F32, "ident")
         vw = [held([P, GW], U32, "vw%d" % c) for c in range(NG)]
         vs = [held([P, GW], U8, "vs%d" % c) for c in range(NG)]
@@ -94,14 +97,14 @@ def tile_list_bridge_board_comparison_kernel(
         def load_w1(q):
             nc.sync.dma_start(out=w1raw[q][:], in_=w1v[:, :, q * NB // 2 : (q + 1) * NB // 2])
 
-        def load_field(gc, m):
-            nc.sync.dma_start(out=fld[gc][m][:], in_=field[m * P : (m + 1) * P, gc * GW : (gc + 1) * GW])
+        def load_field(m):
+            nc.sync.dma_start(out=fld[m][:], in_=field[m * P : (m + 1) * P, :])
 
         def load_page(m):
             nc.sync.dma_start(out=page[m][:], in_=page1[m * P : (m + 1) * P, :])
 
-        def load_wg(gc):
-            nc.sync.dma_start(out=wg[gc][:], in_=wgo[:, gc * GW : (gc + 1) * GW])
+        def load_wg():
+            nc.sync.dma_start(out=wg[:], in_=wgo)
 
         def load_prior():
             with nc.allow_non_contiguous_dma(reason="one value of prior to a partition"):
@@ -118,19 +121,19 @@ def tile_list_bridge_board_comparison_kernel(
         load_tab_rows(1)
         load_tab_rows(2)
         load_tab_rows(3)
-        load_words(tabw, tab_words[0])
+        load_w4()
         load_w1(0)
         load_w1(1)
-        load_w4()
         load_rows(w4s, w4_scales, 0)
         load_rows(w4s, w4_scales, 1)
         load_rows(w4s, w4_scales, 2)
         load_rows(w4s, w4_scales, 3)
+        load_words(tabw, tab_words[0])
         load_w1(2)
         load_w1(3)
-        load_gain()
         nc.sync.dma_start(idx2[:], offs2)
         load_words(tab2w[0], tab2_words[0])
+        load_gain()
         load_rows(tab2s, tab2_scales, 0)
         load_rows(tab2s, tab2_scales, 1)
         load_words(tab2w[1], tab2_words[1])
@@ -139,30 +142,26 @@ def tile_list_bridge_board_comparison_kernel(
         load_words(w8w, w8_words[0])
         load_rows(w8s, w8_scales, 0)
         load_rows(w8s, w8_scales, 1)
-        load_field(0, 0)
+        load_field(0)
         load_rows(w8s, w8_scales, 2)
         load_rows(w8s, w8_scales, 3)
-        load_field(0, 1)
-        load_field(0, 2)
-        load_field(0, 3)
+        load_field(1)
         nc.sync.dma_start(idx3[:], offs3)
-        load_field(1, 0)
+        load_field(2)
         load_prior()
-        load_field(1, 1)
-        load_field(1, 2)
-        load_field(1, 3)
-        load_wg(0)
+        load_field(3)
+        load_wg()
         load_page(0)
         load_page(1)
         load_page(2)
         load_page(3)
-        load_wg(1)
 
         def gather_vs(c):
             nc.vector.tensor_copy(out=vs[c][:], in_=tabs[:].indirect(idx[:, c * GW // 16 : (c + 1) * GW // 16]))
 
         def gather_vw(c):
-            nc.vector.tensor_copy(out=vw[c][:], in_=tabw[:].indirect(idx[:, c * GW // 16 : (c + 1) * GW // 16]))
+            gc, lo = divmod(c * CH, GW)
+            nc.vector.tensor_copy(out=vw[gc][:, lo : lo + CH], in_=tabw[:].indirect(idx[:, c * CH // 16 : (c + 1) * CH // 16]))
 
         def gather_v2w(a):
             nc.vector.tensor_copy(out=v2w[a][:], in_=tab2w[a][:].indirect(idx2[:]))
@@ -171,14 +170,20 @@ def tile_list_bridge_board_comparison_kernel(
             nc.vector.tensor_copy(out=v2s[:], in_=tab2s[:].indirect(idx2[:]))
 
         def cast_w1(q, eng):
-            dst = w1b[q // 2][:, q % 2 * NB // 2 : (q % 2 + 1) * NB // 2, :]
-            src = w1raw[q][:].rearrange("p i r -> p r i")
+            dst = w1b[q // 2][:].rearrange("p (u e m) i -> p u m e i", u=2, e=2)[:, :, q % 2 * P // 2 : (q % 2 + 1) * P // 2]
+            src = w1raw[q][:].rearrange("p i (m u e) -> p u m e i", u=2, e=2)
             if eng == "s":
                 nc.scalar.copy(out=dst, in_=src)
             elif eng == "v":
                 nc.vector.tensor_copy(out=dst, in_=src)
             else:
                 nc.gpsimd.tensor_scalar(out=dst, in0=src, scalar1=1.0, scalar2=0.0, op0=ALU.mult, op1=ALU.add)
+
+        def deal_w4():
+            nc.vector.tensor_copy(out=w4w_d[:].bitcast(U16).rearrange("p (a t m) -> p a t m", a=2, t=4),
+                                  in_=w4w[:].bitcast(U16).rearrange("p (a m t) -> p a t m", a=2, t=4))
+            nc.vector.tensor_copy(out=w4s_d[:].rearrange("p (a t m) -> p a t m", a=2, t=4),
+                                  in_=w4s[:].rearrange("p (a m t) -> p a t m", a=2, t=4))
 
         def quant_w1(a):
             nc.vector.quantize_mx(out=w1q[a][:].bitcast(FP8X4), scales=w1s[a][:], in_=w1b[a][:].rearrange("p r i -> p (r i)"))
@@ -196,30 +201,31 @@ def tile_list_bridge_board_comparison_kernel(
             return banks[-1][:]
 
         ring_a, ring_u, ring_v = ring("bank_a", 2), ring("bank_u", 2), ring("bank_v", 4)
+        ring_y = [held([P, CH], F32, "y%d" % i) for i in range(2)]
         AT, sT, tT = {}, {}, {}
 
         def first(c, a, jl):
             w, sc = deals(c, jl * P, P)
             aT = take(ring_a)
             nc.tensor.matmul_mx(out=aT[:], lhsT=w, lhsT_scale=sc, rhs=w1q[a][:].bitcast(FP8X4), rhs_scale=w1s[a][:], start=True, stop=True)
-            AT[c, a, jl] = work.tile([P, 2, P, 2], F32, name="AT", bufs=12)
-            nc.scalar.copy(out=AT[c, a, jl][:], in_=aT[:].rearrange("j (p u e) -> j u p e", u=2, e=2))
+            AT[c, a, jl] = work.tile([P, NB], F32, name="AT", bufs=12)
+            nc.scalar.copy(out=AT[c, a, jl][:], in_=aT)
 
         def second(c, a, jl):
             w, sc = deals(c, jl * P, P)
             bT = take(ring_v)
-            nc.tensor.matmul_mx(out=bT[:], lhsT=w, lhsT_scale=sc, rhs=w4w[:, 2 * NB * a : 2 * NB * (a + 1)].bitcast(FP4X4),
-                                rhs_scale=w4s[:, NB * a : NB * (a + 1)], start=True, stop=True)
-            sT[c, a, jl] = work.tile([P, 2, P, 2], F32, name="sT", bufs=8)
-            nc.vector.tensor_tensor(out=sT[c, a, jl][:], in0=bT[:].rearrange("j (p u e) -> j u p e", u=2, e=2), in1=AT[c, a, jl][:], op=ALU.add)
+            nc.tensor.matmul_mx(out=bT[:], lhsT=w, lhsT_scale=sc, rhs=w4w_d[:, 2 * NB * a : 2 * NB * (a + 1)].bitcast(FP4X4),
+                                rhs_scale=w4s_d[:, NB * a : NB * (a + 1)], start=True, stop=True)
+            sT[c, a, jl] = work.tile([P, NB], F32, name="sT", bufs=8)
+            nc.vector.tensor_tensor(out=sT[c, a, jl][:], in0=bT, in1=AT[c, a, jl][:], op=ALU.add)
 
         def squash(c, a, jl):
-            tT[c, a, jl] = work.tile([P, 2, P, 2], F32, name="tT", bufs=4)
+            tT[c, a, jl] = work.tile([P, NB], F32, name="tT", bufs=4)
             nc.scalar.activation(out=tT[c, a, jl][:], in_=sT[c, a, jl][:], func=ACT.Tanh)
 
         def turn(dst, c, a, jl, t):
-            nc.tensor.matmul(dst, lhsT=AT[c, a, jl][:, t // 2, :, t % 2], rhs=ident[:], is_transpose=True, start=True, stop=False)
-            nc.tensor.matmul(dst, lhsT=tT[c, a, jl][:, t // 2, :, t % 2], rhs=ident[:], is_transpose=True, start=False, stop=True)
+            nc.tensor.matmul(dst, lhsT=AT[c, a, jl][:, t * P : (t + 1) * P], rhs=ident[:], is_transpose=True, start=True, stop=False)
+            nc.tensor.matmul(dst, lhsT=tT[c, a, jl][:, t * P : (t + 1) * P], rhs=ident[:], is_transpose=True, start=False, stop=True)
 
         def finish(c, a):
             if (c, a) in ON_SCALAR:
@@ -253,7 +259,7 @@ def tile_list_bridge_board_comparison_kernel(
             nc.tensor.matmul_mx(out=d[:], lhsT=w8w[:, mc].bitcast(FP8X4), lhsT_scale=w8s[:, mc],
                                 rhs=vw[gc][:].bitcast(FP8X4), rhs_scale=vs[gc][:], start=True, stop=True)
             df = work.tile([P, GW], F32, name="df", bufs=8)
-            nc.vector.tensor_tensor(out=df[:], in0=d[:], in1=fld[gc][m][:], op=ALU.add)
+            nc.vector.tensor_tensor(out=df[:], in0=d[:], in1=fld[m][:, gc * GW : (gc + 1) * GW], op=ALU.add)
             dfs[gc, m] = df
 
         def score_e(c, pair):
@@ -265,21 +271,18 @@ def tile_list_bridge_board_comparison_kernel(
                                         rhs=hq[c][:, a, :].bitcast(FP8X4), rhs_scale=hs[c][:, a, :], start=(a == 0), stop=(a == 1))
             es[c, pair] = e
 
-        def keep_larger(c, pair):
-            e = es[c, pair]
+        def keep_larger(c, m):
             gc, lo = divmod(c * CH, GW)
-            for i in range(2):
-                m = 2 * pair + i
-                if pair == 1 and c + 1 < NCH:
-                    ys[c, m] = hb[c + 1][:].rearrange("p a n t -> p (a n t)").bitcast(F32)[:, i * CH : (i + 1) * CH]
-                else:
-                    ys[c, m] = work.tile([P, CH], F32, name="y", bufs=4)
-                nc.vector.scalar_tensor_tensor(out=ys[c, m][:], in0=e[:, i, :], scalar=pri[:, m : m + 1], in1=dfs[gc, m][:, lo : lo + CH], op0=ALU.add, op1=ALU.max)
+            if m >= 4 - LATE and c + 1 < NCH and (c, m) != (NCH - 2, 3):
+                ys[c, m] = hb[c + 1][:].rearrange("p a n t -> p (a n t)").bitcast(F32)[:, (3 - m) * CH : (4 - m) * CH]
+            else:
+                ys[c, m] = take(ring_y)
+            nc.vector.scalar_tensor_tensor(out=ys[c, m][:], in0=es[c, m // 2][:, m % 2, :], scalar=pri[:, m : m + 1],
+                                           in1=dfs[gc, m][:, lo : lo + CH], op0=ALU.add, op1=ALU.max)
 
         def put(c, m):
             o = idx3[:, c * CH // 16 : (c + 1) * CH // 16]
-            gc, lo = divmod(c * CH, GW)
-            nc.vector.tensor_tensor(out=page[m][:].indirect(o), in0=ys[c, m][:], in1=wg[gc][:, lo : lo + CH], op=ALU.mult)
+            nc.vector.tensor_tensor(out=page[m][:].indirect(o), in0=ys[c, m][:], in1=wg[:, c * CH : (c + 1) * CH], op=ALU.mult)
             if c == NCH - 1:
                 nc.sync.dma_start(out=out[m * P : (m + 1) * P, :], in_=page[m][:])
 
@@ -287,16 +290,17 @@ def tile_list_bridge_board_comparison_kernel(
 
         gather_vs(0)
         gather_vs(1)
-        gather_vw(0)
         cast_w1(0, "s")
-        gather_vw(1)
         cast_w1(1, "s")
+        deal_w4()
         quant_w1(0)
+        for c in range(NCH):
+            gather_vw(c)
         for jl in range(JT):
             first(0, 0, jl)
             second(0, 0, jl)
-        cast_w1(2, "s")
-        cast_w1(3, "v")
+        cast_w1(2, "v")
+        cast_w1(3, "s")
         for jl in range(JT):
             first(1, 0, jl)
             second(1, 0, jl)
@@ -308,7 +312,7 @@ def tile_list_bridge_board_comparison_kernel(
         gather_v2w(0)
         gather_v2w(1)
         gather_v2s()
-        D_AT = {0: [(0, 0), (0, 1), (0, 2), (0, 3)], 1: [(1, 0), (1, 1), (1, 2), (1, 3)]}
+        D_AT = {0: [(gc, m) for gc in range(2) for m in range(4)]}
         for c in range(NCH):
             for a in range(2):
                 for jl in range(JT):
@@ -316,22 +320,30 @@ def tile_list_bridge_board_comparison_kernel(
             for a in range(2):
                 finish(c, a)
             quant_h(c)
-            if c > 0:
-                keep_larger(c - 1, 1)
+            if c + 1 == NCH:
+                break
+            late = [(c - 1, m) for m in range(4 - LATE, 4)] if c > 0 else []
+            for cm in late:
+                keep_larger(*cm)
             if c + 2 < NCH:
                 for a, jl in units:
                     first(c + 2, a, jl)
                     second(c + 2, a, jl)
             for gc, m in D_AT.get(c, []):
                 score_d(gc, m)
-            score_e(c, 0)
-            score_e(c, 1)
-            if c > 0:
-                put(c - 1, 2)
-                put(c - 1, 3)
-            keep_larger(c, 0)
-            put(c, 0)
-            put(c, 1)
-        keep_larger(NCH - 1, 1)
-        put(NCH - 1, 2)
-        put(NCH - 1, 3)
+            for pair in range(2):
+                score_e(c, pair)
+            for cm in late:
+                put(*cm)
+            for m in range(4 - LATE):
+                keep_larger(c, m)
+            for m in range(4 - LATE):
+                put(c, m)
+        steps = [(2, 2), (3, 2), (3, 0), (2, 3), (3, 3), (3, 1)]
+        for pair in (1, 0):
+            score_e(NCH - 1, pair)
+        keep_larger(*steps[0])
+        for i, cm in enumerate(steps):
+            if i + 1 < len(steps):
+                keep_larger(*steps[i + 1])
+            put(*cm)

@@ -54,8 +54,6 @@ def tile_list_bridge_board_comparison_kernel(
         w1s = [held([P, NB], U8, "w1s%d" % a) for a in range(2)]
         w4w = held([P, 2 * H], U8, "w4w")
         w4s = held([P, H], U8, "w4s")
-        w4w_d = held([P, 2 * H], U8, "w4w_d")
-        w4s_d = held([P, H], U8, "w4s_d")
         w8w = held([P, S2], U32, "w8w")
         w8s = held([P, S2], U8, "w8s")
         g = held([P, 2, 4], F32, "g")
@@ -64,8 +62,8 @@ def tile_list_bridge_board_comparison_kernel(
         page = [held([P, T2], F32, "page%d" % m) for m in range(4)]
         wg = held([P, S], F32, "wg")
         ident = held([P, P], F32, "ident")
-        vw = [held([P, GW], U32, "vw%d" % c) for c in range(NG)]
-        vs = [held([P, GW], U8, "vs%d" % c) for c in range(NG)]
+        vw = held([P, S], U32, "vw")
+        vs = held([P, S], U8, "vs")
         v2w = [held([P, S2], U32, "v2w%d" % a) for a in range(2)]
         v2s = held([P, S2], U8, "v2s")
         hb = [held([P, 2, CH, 4], BF16, "hb%d" % c) for c in range(NCH)]
@@ -121,14 +119,14 @@ def tile_list_bridge_board_comparison_kernel(
         load_tab_rows(1)
         load_tab_rows(2)
         load_tab_rows(3)
-        load_w4()
         load_w1(0)
         load_w1(1)
+        load_words(tabw, tab_words[0])
         load_rows(w4s, w4_scales, 0)
         load_rows(w4s, w4_scales, 1)
         load_rows(w4s, w4_scales, 2)
         load_rows(w4s, w4_scales, 3)
-        load_words(tabw, tab_words[0])
+        load_w4()
         load_w1(2)
         load_w1(3)
         nc.sync.dma_start(idx2[:], offs2)
@@ -156,12 +154,11 @@ def tile_list_bridge_board_comparison_kernel(
         load_page(2)
         load_page(3)
 
-        def gather_vs(c):
-            nc.vector.tensor_copy(out=vs[c][:], in_=tabs[:].indirect(idx[:, c * GW // 16 : (c + 1) * GW // 16]))
+        def gather_vs():
+            nc.vector.tensor_copy(out=vs[:], in_=tabs[:].indirect(idx[:]))
 
-        def gather_vw(c):
-            gc, lo = divmod(c * CH, GW)
-            nc.vector.tensor_copy(out=vw[gc][:, lo : lo + CH], in_=tabw[:].indirect(idx[:, c * CH // 16 : (c + 1) * CH // 16]))
+        def gather_vw(lo, hi):
+            nc.vector.tensor_copy(out=vw[:, lo:hi], in_=tabw[:].indirect(idx[:, lo // 16 : hi // 16]))
 
         def gather_v2w(a):
             nc.vector.tensor_copy(out=v2w[a][:], in_=tab2w[a][:].indirect(idx2[:]))
@@ -170,8 +167,8 @@ def tile_list_bridge_board_comparison_kernel(
             nc.vector.tensor_copy(out=v2s[:], in_=tab2s[:].indirect(idx2[:]))
 
         def cast_w1(q, eng):
-            dst = w1b[q // 2][:].rearrange("p (u e m) i -> p u m e i", u=2, e=2)[:, :, q % 2 * P // 2 : (q % 2 + 1) * P // 2]
-            src = w1raw[q][:].rearrange("p i (m u e) -> p u m e i", u=2, e=2)
+            dst = w1b[q // 2][:, q % 2 * NB // 2 : (q % 2 + 1) * NB // 2, :]
+            src = w1raw[q][:].rearrange("p i r -> p r i")
             if eng == "s":
                 nc.scalar.copy(out=dst, in_=src)
             elif eng == "v":
@@ -179,19 +176,12 @@ def tile_list_bridge_board_comparison_kernel(
             else:
                 nc.gpsimd.tensor_scalar(out=dst, in0=src, scalar1=1.0, scalar2=0.0, op0=ALU.mult, op1=ALU.add)
 
-        def deal_w4():
-            nc.vector.tensor_copy(out=w4w_d[:].bitcast(U16).rearrange("p (a t m) -> p a t m", a=2, t=4),
-                                  in_=w4w[:].bitcast(U16).rearrange("p (a m t) -> p a t m", a=2, t=4))
-            nc.vector.tensor_copy(out=w4s_d[:].rearrange("p (a t m) -> p a t m", a=2, t=4),
-                                  in_=w4s[:].rearrange("p (a m t) -> p a t m", a=2, t=4))
-
         def quant_w1(a):
             nc.vector.quantize_mx(out=w1q[a][:].bitcast(FP8X4), scales=w1s[a][:], in_=w1b[a][:].rearrange("p r i -> p (r i)"))
 
         def deals(c, lo, n):
             j0 = c * CH + lo
-            cols = slice(j0 % GW, j0 % GW + n)
-            return vw[j0 // GW][:, cols].bitcast(FP8X4), vs[j0 // GW][:, cols]
+            return vw[:, j0 : j0 + n].bitcast(FP8X4), vs[:, j0 : j0 + n]
 
         def ring(name, n):
             return [psum.tile([P, NB], F32, name="%s%d" % (name, i)) for i in range(n)]
@@ -209,15 +199,16 @@ def tile_list_bridge_board_comparison_kernel(
             aT = take(ring_a)
             nc.tensor.matmul_mx(out=aT[:], lhsT=w, lhsT_scale=sc, rhs=w1q[a][:].bitcast(FP8X4), rhs_scale=w1s[a][:], start=True, stop=True)
             AT[c, a, jl] = work.tile([P, NB], F32, name="AT", bufs=12)
-            nc.scalar.copy(out=AT[c, a, jl][:], in_=aT)
+            nc.scalar.copy(out=AT[c, a, jl][:].rearrange("j (t p) -> j t p", t=4), in_=aT.rearrange("j (p t) -> j t p", t=4))
 
         def second(c, a, jl):
             w, sc = deals(c, jl * P, P)
             bT = take(ring_v)
-            nc.tensor.matmul_mx(out=bT[:], lhsT=w, lhsT_scale=sc, rhs=w4w_d[:, 2 * NB * a : 2 * NB * (a + 1)].bitcast(FP4X4),
-                                rhs_scale=w4s_d[:, NB * a : NB * (a + 1)], start=True, stop=True)
+            nc.tensor.matmul_mx(out=bT[:], lhsT=w, lhsT_scale=sc, rhs=w4w[:, 2 * NB * a : 2 * NB * (a + 1)].bitcast(FP4X4),
+                                rhs_scale=w4s[:, NB * a : NB * (a + 1)], start=True, stop=True)
             sT[c, a, jl] = work.tile([P, NB], F32, name="sT", bufs=8)
-            nc.vector.tensor_tensor(out=sT[c, a, jl][:], in0=bT, in1=AT[c, a, jl][:], op=ALU.add)
+            nc.vector.tensor_tensor(out=sT[c, a, jl][:].rearrange("j (t p) -> j t p", t=4), in0=bT.rearrange("j (p t) -> j t p", t=4),
+                                        in1=AT[c, a, jl][:].rearrange("j (t p) -> j t p", t=4), op=ALU.add)
 
         def squash(c, a, jl):
             tT[c, a, jl] = work.tile([P, NB], F32, name="tT", bufs=4)
@@ -238,7 +229,7 @@ def tile_list_bridge_board_comparison_kernel(
                     for t in range(2):
                         nc.scalar.activation(out=flat[:, 2 * half + t, :], in_=U[:, t, :], func=ACT.Copy,
                                              scale=g[:, a, 2 * half + t : 2 * half + t + 1])
-                nc.scalar.copy(out=hb[c][:, a], in_=flat[:].rearrange("p t n -> p n t"))
+                nc.scalar.copy(out=hb[c][:, a].rearrange("p (n i) t -> p n t i", i=4), in_=flat[:].rearrange("p t (n i) -> p n t i", i=4))
             else:
                 for jl in range(JT):
                     U = take(ring_u).rearrange("p (t n) -> p t n", t=4)
@@ -257,7 +248,7 @@ def tile_list_bridge_board_comparison_kernel(
             mc = slice(m * P, (m + 1) * P)
             d = take(ring_v)
             nc.tensor.matmul_mx(out=d[:], lhsT=w8w[:, mc].bitcast(FP8X4), lhsT_scale=w8s[:, mc],
-                                rhs=vw[gc][:].bitcast(FP8X4), rhs_scale=vs[gc][:], start=True, stop=True)
+                                rhs=vw[:, gc * GW : (gc + 1) * GW].bitcast(FP8X4), rhs_scale=vs[:, gc * GW : (gc + 1) * GW], start=True, stop=True)
             df = work.tile([P, GW], F32, name="df", bufs=8)
             nc.vector.tensor_tensor(out=df[:], in0=d[:], in1=fld[m][:, gc * GW : (gc + 1) * GW], op=ALU.add)
             dfs[gc, m] = df
@@ -288,14 +279,12 @@ def tile_list_bridge_board_comparison_kernel(
 
         units = [(a, jl) for a in range(2) for jl in range(JT)]
 
-        gather_vs(0)
-        gather_vs(1)
+        gather_vs()
         cast_w1(0, "s")
         cast_w1(1, "s")
-        deal_w4()
         quant_w1(0)
-        for c in range(NCH):
-            gather_vw(c)
+        gather_vw(0, CH)
+        gather_vw(CH, S)
         for jl in range(JT):
             first(0, 0, jl)
             second(0, 0, jl)

@@ -18,14 +18,18 @@ ALU = mybir.AluOpType
 ACT = mybir.ActivationFunctionType
 
 P = 128
-NB = 512
-CH = 256
-NCH = S // CH
-GW = 512
-NG = S // GW
-JT = CH // P
-LATE = 2
-ON_SCALAR = ((0, 0), (1, 0), (1, 1), (2, 0), (2, 1), (3, 0), (3, 1))
+PACK = 4
+BANK = 512
+PASSES = H // BANK
+W1_PIECE = BANK // 2
+CHUNK = 256
+CHUNKS = S // CHUNK
+TILES = CHUNK // P
+HALVES = S // BANK
+M_TILES = S2 // P
+EARLY, LATE = (0, 1), (2, 3)
+AHEAD = 2
+GAIN_ON_VECTOR = (0, 1)
 
 
 def tile_list_bridge_board_comparison_kernel(
@@ -35,7 +39,7 @@ def tile_list_bridge_board_comparison_kernel(
     nc = tc.nc
     with ExitStack() as ctx:
         keep = ctx.enter_context(tc.tile_pool(name="keep", bufs=1))
-        work = ctx.enter_context(tc.tile_pool(name="work", bufs=3))
+        work = ctx.enter_context(tc.tile_pool(name="work", bufs=1))
         psum = ctx.enter_context(tc.psum_pool(name="psum", bufs=1))
 
         def held(shape, dtype, name):
@@ -44,295 +48,253 @@ def tile_list_bridge_board_comparison_kernel(
         idx = held([P, S // 16], U16, "idx")
         idx2 = held([P, S2 // 16], U16, "idx2")
         idx3 = held([P, S // 16], U16, "idx3")
-        tabw = held([P, T], U32, "tabw")
-        tabs = held([P, T], U8, "tabs")
-        tab2w = [held([P, T3], U32, "tab2w%d" % a) for a in range(2)]
-        tab2s = held([P, T3], U8, "tab2s")
-        w1raw = [held([P, 4, NB // 2], F32, "w1raw%d" % a) for a in range(4)]
-        w1b = [held([P, NB, 4], BF16, "w1b")] * 2
-        w1q = [held([P, NB], U32, "w1q%d" % a) for a in range(2)]
-        w1s = [held([P, NB], U8, "w1s%d" % a) for a in range(2)]
-        w4w = held([P, 2 * H], U8, "w4w")
-        w4s = held([P, H], U8, "w4s")
-        w8w = held([P, S2], U32, "w8w")
-        w8s = held([P, S2], U8, "w8s")
-        g = held([P, 2, 4], F32, "g")
-        pri = held([P, 4], F32, "pri")
-        fld = [held([P, S], F32, "fld%d" % m) for m in range(4)]
-        page = [held([P, T2], F32, "page%d" % m) for m in range(4)]
-        wg = held([P, S], F32, "wg")
+        tab_w = held([P, T], U32, "tab_w")
+        tab_s = held([P, T], U8, "tab_s")
+        tab2_w = [held([P, T3], U32, "tab2_w%d" % g) for g in range(PASSES)]
+        tab2_s = held([P, T3], U8, "tab2_s")
+        w1_raw = [held([P, PACK, W1_PIECE], F32, "w1_raw%d" % q) for q in range(H // W1_PIECE)]
+        w1_bf = held([P, BANK, PACK], BF16, "w1_bf")
+        w1_w = [held([P, BANK], U32, "w1_w%d" % g) for g in range(PASSES)]
+        w1_s = [held([P, BANK], U8, "w1_s%d" % g) for g in range(PASSES)]
+        w4_w = held([P, 2 * H], U8, "w4_w")
+        w4_s = held([P, H], U8, "w4_s")
+        w8_w = held([P, S2], U32, "w8_w")
+        w8_s = held([P, S2], U8, "w8_s")
+        gain_sb = held([P, PASSES, PACK], F32, "gain_sb")
+        prior_sb = held([P, M_TILES], F32, "prior_sb")
+        field_sb = [held([P, S], F32, "field_sb%d" % m) for m in range(M_TILES)]
+        page = [held([P, T2], F32, "page%d" % m) for m in range(M_TILES)]
+        wgo_sb = held([P, S], F32, "wgo_sb")
         ident = held([P, P], F32, "ident")
-        vw = held([P, S], U32, "vw")
-        vs = held([P, S], U8, "vs")
-        v2w = [held([P, S2], U32, "v2w%d" % a) for a in range(2)]
-        v2s = held([P, S2], U8, "v2s")
-        hb = [held([P, 2, CH, 4], BF16, "hb%d" % c) for c in range(NCH)]
-        hq = [held([P, 2, CH], U32, "hq%d" % c) for c in range(NCH)]
-        hs = [held([P, 2, CH], U8, "hs%d" % c) for c in range(NCH)]
+        v_w = [held([P, BANK], U32, "v_w%d" % half) for half in range(HALVES)]
+        v_s = [held([P, BANK], U8, "v_s%d" % half) for half in range(HALVES)]
+        v2_w = [held([P, S2], U32, "v2_w%d" % g) for g in range(PASSES)]
+        v2_s = held([P, S2], U8, "v2_s")
+        h_bf = [held([P, PASSES, CHUNK, PACK], BF16, "h_bf%d" % c) for c in range(CHUNKS)]
+        h_w = [held([P, PASSES, CHUNK], U32, "h_w%d" % c) for c in range(CHUNKS)]
+        h_s = [held([P, PASSES, CHUNK], U8, "h_s%d" % c) for c in range(CHUNKS)]
 
-        for plane in (w4s, tab2s, w8s):
-            nc.vector.memset(plane[:].bitcast(I32), 0)
+        for scale_tile in (tab_s, w4_s, tab2_s, w8_s):
+            nc.vector.memset(scale_tile[:].bitcast(I32), 0)
         make_identity(nc, ident[:])
 
-        def load_rows(plane, dram, q):
-            passes = dram.shape[0]
-            nc.sync.dma_start(
-                out=plane[32 * q : 32 * q + 4 * passes, :].bitcast(I32),
-                in_=dram[:, 4 * q : 4 * q + 4, :].bitcast(I32),
-            )
-
-        def load_tab_rows(q):
-            nc.sync.dma_start(
-                out=tabs[32 * q : 32 * q + 32, :].bitcast(I32),
-                in_=tab_scales[:, 4 * q : 4 * q + 4, :].bitcast(I32).to_broadcast([8, 4, T // 4]),
-            )
+        def load_scales(scale_tile, dram, groups):
+            rows = 4 * dram.shape[0]
+            for q in groups:
+                nc.sync.dma_start(out=scale_tile[32 * q : 32 * q + rows, :].bitcast(I32), in_=dram[:, 4 * q : 4 * q + 4, :].bitcast(I32))
 
         def load_words(tile, dram):
             nc.sync.dma_start(out=tile[:].bitcast(I32), in_=dram.rearrange("p t i -> p (t i)").bitcast(I32))
 
-        w1v = w1.rearrange("(p i) r -> p i r", i=4)
-
         def load_w1(q):
-            nc.sync.dma_start(out=w1raw[q][:], in_=w1v[:, :, q * NB // 2 : (q + 1) * NB // 2])
+            by_partition = w1.rearrange("(p i) r -> p i r", i=PACK)
+            nc.sync.dma_start(out=w1_raw[q][:], in_=by_partition[:, :, q * W1_PIECE : (q + 1) * W1_PIECE])
 
         def load_field(m):
-            nc.sync.dma_start(out=fld[m][:], in_=field[m * P : (m + 1) * P, :])
-
-        def load_page(m):
-            nc.sync.dma_start(out=page[m][:], in_=page1[m * P : (m + 1) * P, :])
-
-        def load_wg():
-            nc.sync.dma_start(out=wg[:], in_=wgo)
-
-        def load_prior():
-            with nc.allow_non_contiguous_dma(reason="one value of prior to a partition"):
-                nc.sync.dma_start(out=pri[:], in_=prior.rearrange("(m p) -> p m", p=P))
-
-        def load_gain():
-            nc.sync.dma_start(out=g[:], in_=gain.rearrange("(a p t) -> p a t", a=2, t=4))
-
-        def load_w4():
-            nc.sync.dma_start(out=w4w[:].bitcast(I32), in_=w4_words[0].bitcast(I32))
+            nc.sync.dma_start(out=field_sb[m][:], in_=field[m * P : (m + 1) * P, :])
 
         nc.sync.dma_start(idx[:], offs)
-        load_tab_rows(0)
-        load_tab_rows(1)
-        load_tab_rows(2)
-        load_tab_rows(3)
+        load_scales(tab_s, tab_scales, range(4))
+        nc.sync.dma_start(out=w4_w[:].bitcast(I32), in_=w4_words[0].bitcast(I32))
         load_w1(0)
         load_w1(1)
-        load_words(tabw, tab_words[0])
-        load_rows(w4s, w4_scales, 0)
-        load_rows(w4s, w4_scales, 1)
-        load_rows(w4s, w4_scales, 2)
-        load_rows(w4s, w4_scales, 3)
-        load_w4()
+        load_scales(w4_s, w4_scales, range(4))
+        load_words(tab_w, tab_words[0])
         load_w1(2)
         load_w1(3)
         nc.sync.dma_start(idx2[:], offs2)
-        load_words(tab2w[0], tab2_words[0])
-        load_gain()
-        load_rows(tab2s, tab2_scales, 0)
-        load_rows(tab2s, tab2_scales, 1)
-        load_words(tab2w[1], tab2_words[1])
-        load_rows(tab2s, tab2_scales, 2)
-        load_rows(tab2s, tab2_scales, 3)
-        load_words(w8w, w8_words[0])
-        load_rows(w8s, w8_scales, 0)
-        load_rows(w8s, w8_scales, 1)
+        load_words(tab2_w[0], tab2_words[0])
+        nc.sync.dma_start(out=gain_sb[:], in_=gain.rearrange("(g p t) -> p g t", g=PASSES, t=PACK))
+        load_scales(tab2_s, tab2_scales, (0, 1))
+        load_words(tab2_w[1], tab2_words[1])
+        load_scales(tab2_s, tab2_scales, (2, 3))
+        load_words(w8_w, w8_words[0])
+        load_scales(w8_s, w8_scales, (0, 1))
         load_field(0)
-        load_rows(w8s, w8_scales, 2)
-        load_rows(w8s, w8_scales, 3)
+        load_scales(w8_s, w8_scales, (2, 3))
         load_field(1)
         nc.sync.dma_start(idx3[:], offs3)
         load_field(2)
-        load_prior()
+        with nc.allow_non_contiguous_dma(reason="four values of prior to a partition"):
+            nc.sync.dma_start(out=prior_sb[:], in_=prior.rearrange("(m p) -> p m", p=P))
         load_field(3)
-        load_wg()
-        load_page(0)
-        load_page(1)
-        load_page(2)
-        load_page(3)
+        nc.sync.dma_start(out=wgo_sb[:], in_=wgo)
+        for m in range(M_TILES):
+            nc.sync.dma_start(out=page[m][:], in_=page1[m * P : (m + 1) * P, :])
 
-        def gather_vs():
-            nc.vector.tensor_copy(out=vs[:], in_=tabs[:].indirect(idx[:]))
+        def entries(index_tile, first, count):
+            return index_tile[:, first // 16 : (first + count) // 16]
 
-        def gather_vw(lo, hi):
-            nc.vector.tensor_copy(out=vw[:, lo:hi], in_=tabw[:].indirect(idx[:, lo // 16 : hi // 16]))
+        def round_w1(q, copy):
+            lo = q * W1_PIECE % BANK
+            copy(out=w1_bf[:, lo : lo + W1_PIECE, :], in_=w1_raw[q][:].rearrange("p i r -> p r i"))
 
-        def gather_v2w(a):
-            nc.vector.tensor_copy(out=v2w[a][:], in_=tab2w[a][:].indirect(idx2[:]))
+        def quantise_w1(g):
+            nc.vector.quantize_mx(out=w1_w[g][:].bitcast(FP8X4), scales=w1_s[g][:], in_=w1_bf[:].rearrange("p r i -> p (r i)"))
 
-        def gather_v2s():
-            nc.vector.tensor_copy(out=v2s[:], in_=tab2s[:].indirect(idx2[:]))
+        def deals(c, jt):
+            half, lo = divmod(c * CHUNK + jt * P, BANK)
+            return v_w[half][:, lo : lo + P].bitcast(FP8X4), v_s[half][:, lo : lo + P]
 
-        def cast_w1(q, eng):
-            dst = w1b[q // 2][:, q % 2 * NB // 2 : (q % 2 + 1) * NB // 2, :]
-            src = w1raw[q][:].rearrange("p i r -> p r i")
-            if eng == "s":
-                nc.scalar.copy(out=dst, in_=src)
-            elif eng == "v":
-                nc.vector.tensor_copy(out=dst, in_=src)
-            else:
-                nc.gpsimd.tensor_scalar(out=dst, in0=src, scalar1=1.0, scalar2=0.0, op0=ALU.mult, op1=ALU.add)
+        def banks(name, count):
+            return [psum.tile([P, BANK], F32, name="%s%d" % (name, i)) for i in range(count)]
 
-        def quant_w1(a):
-            nc.vector.quantize_mx(out=w1q[a][:].bitcast(FP8X4), scales=w1s[a][:], in_=w1b[a][:].rearrange("p r i -> p (r i)"))
+        def take(ring):
+            ring.append(ring.pop(0))
+            return ring[-1][:]
 
-        def deals(c, lo, n):
-            j0 = c * CH + lo
-            return vw[:, j0 : j0 + n].bitcast(FP8X4), vs[:, j0 : j0 + n]
+        a_banks = banks("a_bank", 2)
+        sum_banks = banks("sum_bank", 2)
+        vector_banks = banks("vector_bank", 4)
+        y_ring = [held([P, CHUNK], F32, "y%d" % i) for i in range(2)]
+        per_chunk = PASSES * TILES
+        a_sb, ab_sb, tanh_sb, d_sb, e_ps, y_sb = {}, {}, {}, {}, {}, {}
 
-        def ring(name, n):
-            return [psum.tile([P, NB], F32, name="%s%d" % (name, i)) for i in range(n)]
+        def by_t(tile):
+            return tile[:].rearrange("j (t p) -> j t p", t=PACK)
 
-        def take(banks):
-            banks.append(banks.pop(0))
-            return banks[-1][:]
+        def bank_by_t(bank):
+            return bank.rearrange("j (p t) -> j t p", t=PACK)
 
-        ring_a, ring_u, ring_v = ring("bank_a", 2), ring("bank_u", 2), ring("bank_v", 4)
-        ring_y = [held([P, CH], F32, "y%d" % i) for i in range(2)]
-        AT, sT, tT = {}, {}, {}
+        def make_a_and_sum(c, g, jt):
+            words, scales = deals(c, jt)
+            key = (c, g, jt)
+            a_ps = take(a_banks)
+            nc.tensor.matmul_mx(out=a_ps, lhsT=words, lhsT_scale=scales, rhs=w1_w[g][:].bitcast(FP8X4), rhs_scale=w1_s[g][:],
+                                start=True, stop=True)
+            a_sb[key] = work.tile([P, BANK], F32, name="a_sb", bufs=(AHEAD + 1) * per_chunk)
+            nc.scalar.copy(out=by_t(a_sb[key]), in_=bank_by_t(a_ps))
+            b_ps = take(vector_banks)
+            nc.tensor.matmul_mx(out=b_ps, lhsT=words, lhsT_scale=scales,
+                                rhs=w4_w[:, 2 * BANK * g : 2 * BANK * (g + 1)].bitcast(FP4X4),
+                                rhs_scale=w4_s[:, BANK * g : BANK * (g + 1)], start=True, stop=True)
+            ab_sb[key] = work.tile([P, BANK], F32, name="ab_sb", bufs=AHEAD * per_chunk)
+            nc.vector.tensor_tensor(out=by_t(ab_sb[key]), in0=bank_by_t(b_ps), in1=by_t(a_sb[key]), op=ALU.add)
 
-        def first(c, a, jl):
-            w, sc = deals(c, jl * P, P)
-            aT = take(ring_a)
-            nc.tensor.matmul_mx(out=aT[:], lhsT=w, lhsT_scale=sc, rhs=w1q[a][:].bitcast(FP8X4), rhs_scale=w1s[a][:], start=True, stop=True)
-            AT[c, a, jl] = work.tile([P, NB], F32, name="AT", bufs=12)
-            nc.scalar.copy(out=AT[c, a, jl][:].rearrange("j (t p) -> j t p", t=4), in_=aT.rearrange("j (p t) -> j t p", t=4))
+        def make_tanh(c, g, jt):
+            tanh_sb[c, g, jt] = work.tile([P, BANK], F32, name="tanh_sb", bufs=per_chunk)
+            nc.scalar.activation(out=tanh_sb[c, g, jt][:], in_=ab_sb[c, g, jt][:], func=ACT.Tanh)
 
-        def second(c, a, jl):
-            w, sc = deals(c, jl * P, P)
-            bT = take(ring_v)
-            nc.tensor.matmul_mx(out=bT[:], lhsT=w, lhsT_scale=sc, rhs=w4w[:, 2 * NB * a : 2 * NB * (a + 1)].bitcast(FP4X4),
-                                rhs_scale=w4s[:, NB * a : NB * (a + 1)], start=True, stop=True)
-            sT[c, a, jl] = work.tile([P, NB], F32, name="sT", bufs=8)
-            nc.vector.tensor_tensor(out=sT[c, a, jl][:].rearrange("j (t p) -> j t p", t=4), in0=bT.rearrange("j (p t) -> j t p", t=4),
-                                        in1=AT[c, a, jl][:].rearrange("j (t p) -> j t p", t=4), op=ALU.add)
+        def turn_and_add(dst, c, g, jt, t):
+            cols = slice(t * P, (t + 1) * P)
+            nc.tensor.matmul(dst, lhsT=a_sb[c, g, jt][:, cols], rhs=ident[:], is_transpose=True, start=True, stop=False)
+            nc.tensor.matmul(dst, lhsT=tanh_sb[c, g, jt][:, cols], rhs=ident[:], is_transpose=True, start=False, stop=True)
 
-        def squash(c, a, jl):
-            tT[c, a, jl] = work.tile([P, NB], F32, name="tT", bufs=4)
-            nc.scalar.activation(out=tT[c, a, jl][:], in_=sT[c, a, jl][:], func=ACT.Tanh)
+        def finish_h_on_scalar(c, g):
+            h_by_t = work.tile([P, PACK, CHUNK], BF16, name="h_by_t", bufs=PASSES)
+            per_bank = BANK // CHUNK
+            for t0 in range(0, PACK, per_bank):
+                sums = take(sum_banks).rearrange("p (t n) -> p t n", t=per_bank)
+                for t in range(t0, t0 + per_bank):
+                    for jt in range(TILES):
+                        turn_and_add(sums[:, t - t0, jt * P : (jt + 1) * P], c, g, jt, t)
+                for t in range(t0, t0 + per_bank):
+                    nc.scalar.activation(out=h_by_t[:, t, :], in_=sums[:, t - t0, :], func=ACT.Copy, scale=gain_sb[:, g, t : t + 1])
+            nc.scalar.copy(out=h_bf[c][:, g].rearrange("p (n i) t -> p n t i", i=4), in_=h_by_t[:].rearrange("p t (n i) -> p n t i", i=4))
 
-        def turn(dst, c, a, jl, t):
-            nc.tensor.matmul(dst, lhsT=AT[c, a, jl][:, t * P : (t + 1) * P], rhs=ident[:], is_transpose=True, start=True, stop=False)
-            nc.tensor.matmul(dst, lhsT=tT[c, a, jl][:, t * P : (t + 1) * P], rhs=ident[:], is_transpose=True, start=False, stop=True)
+        def finish_h_on_vector(c, g):
+            for jt in range(TILES):
+                sums = take(sum_banks).rearrange("p (t n) -> p t n", t=PACK)
+                for t in range(PACK):
+                    turn_and_add(sums[:, t, :], c, g, jt, t)
+                nc.vector.tensor_tensor(out=h_bf[c][:, g, jt * P : (jt + 1) * P, :], in0=sums.rearrange("p t n -> p n t"),
+                                        in1=gain_sb[:, g, :].unsqueeze(1).to_broadcast([P, P, PACK]), op=ALU.mult)
 
-        def finish(c, a):
-            if (c, a) in ON_SCALAR:
-                flat = work.tile([P, 4, CH], BF16, name="flat", bufs=2)
-                for half in range(2):
-                    U = take(ring_u).rearrange("p (t n) -> p t n", t=2)
-                    for t in range(2):
-                        for jl in range(JT):
-                            turn(U[:, t, jl * P : (jl + 1) * P], c, a, jl, 2 * half + t)
-                    for t in range(2):
-                        nc.scalar.activation(out=flat[:, 2 * half + t, :], in_=U[:, t, :], func=ACT.Copy,
-                                             scale=g[:, a, 2 * half + t : 2 * half + t + 1])
-                nc.scalar.copy(out=hb[c][:, a].rearrange("p (n i) t -> p n t i", i=4), in_=flat[:].rearrange("p t (n i) -> p n t i", i=4))
-            else:
-                for jl in range(JT):
-                    U = take(ring_u).rearrange("p (t n) -> p t n", t=4)
-                    for t in range(4):
-                        turn(U[:, t, :], c, a, jl, t)
-                    nc.vector.tensor_tensor(out=hb[c][:, a, jl * P : (jl + 1) * P, :], in0=U[:].rearrange("p t n -> p n t"),
-                                            in1=g[:, a, :].unsqueeze(1).to_broadcast([P, P, 4]), op=ALU.mult)
+        def make_h(c):
+            for g in range(PASSES):
+                for jt in range(TILES):
+                    make_tanh(c, g, jt)
+            for g in range(PASSES):
+                finish = finish_h_on_vector if (c, g) == GAIN_ON_VECTOR else finish_h_on_scalar
+                finish(c, g)
+            nc.vector.quantize_mx(out=h_w[c][:].rearrange("p g n -> p (g n)").bitcast(FP8X4), scales=h_s[c][:].rearrange("p g n -> p (g n)"),
+                                  in_=h_bf[c][:].rearrange("p g n t -> p (g n t)"))
 
-        def quant_h(c):
-            nc.vector.quantize_mx(out=hq[c][:].rearrange("p a n -> p (a n)").bitcast(FP8X4), scales=hs[c][:].rearrange("p a n -> p (a n)"),
-                                  in_=hb[c][:].rearrange("p a n t -> p (a n t)"))
+        def make_d(half, m):
+            cols = slice(m * P, (m + 1) * P)
+            d_ps = take(vector_banks)
+            nc.tensor.matmul_mx(out=d_ps, lhsT=w8_w[:, cols].bitcast(FP8X4), lhsT_scale=w8_s[:, cols],
+                                rhs=v_w[half][:].bitcast(FP8X4), rhs_scale=v_s[half][:], start=True, stop=True)
+            d_sb[half, m] = work.tile([P, BANK], F32, name="d_sb", bufs=HALVES * M_TILES)
+            nc.vector.tensor_tensor(out=d_sb[half, m][:], in0=d_ps, in1=field_sb[m][:, half * BANK : (half + 1) * BANK], op=ALU.add)
 
-        ys, dfs, es = {}, {}, {}
+        def make_e(c, pair):
+            bank = take(vector_banks).rearrange("p (i n) -> p i n", i=len(pair))
+            for i, m in enumerate(pair):
+                cols = slice(m * P, (m + 1) * P)
+                for g in range(PASSES):
+                    nc.tensor.matmul_mx(out=bank[:, i, :], lhsT=v2_w[g][:, cols].bitcast(FP8X4), lhsT_scale=v2_s[4 * g : P, cols],
+                                        rhs=h_w[c][:, g, :].bitcast(FP8X4), rhs_scale=h_s[c][:, g, :],
+                                        start=(g == 0), stop=(g == PASSES - 1))
+                e_ps[c, m] = bank[:, i, :]
 
-        def score_d(gc, m):
-            mc = slice(m * P, (m + 1) * P)
-            d = take(ring_v)
-            nc.tensor.matmul_mx(out=d[:], lhsT=w8w[:, mc].bitcast(FP8X4), lhsT_scale=w8s[:, mc],
-                                rhs=vw[:, gc * GW : (gc + 1) * GW].bitcast(FP8X4), rhs_scale=vs[:, gc * GW : (gc + 1) * GW], start=True, stop=True)
-            df = work.tile([P, GW], F32, name="df", bufs=8)
-            nc.vector.tensor_tensor(out=df[:], in0=d[:], in1=fld[m][:, gc * GW : (gc + 1) * GW], op=ALU.add)
-            dfs[gc, m] = df
+        def spent_h(c, m):
+            slot = M_TILES - 1 - m
+            return h_bf[c][:].rearrange("p g n t -> p (g n t)").bitcast(F32)[:, slot * CHUNK : (slot + 1) * CHUNK]
 
-        def score_e(c, pair):
-            e = take(ring_v).rearrange("p (i n) -> p i n", i=2)
-            for i in range(2):
-                mc = slice((2 * pair + i) * P, (2 * pair + i + 1) * P)
-                for a in range(2):
-                    nc.tensor.matmul_mx(out=e[:, i, :], lhsT=v2w[a][:, mc].bitcast(FP8X4), lhsT_scale=v2s[4 * a : P, mc],
-                                        rhs=hq[c][:, a, :].bitcast(FP8X4), rhs_scale=hs[c][:, a, :], start=(a == 0), stop=(a == 1))
-            es[c, pair] = e
+        def make_y(c, m, dst):
+            half, lo = divmod(c * CHUNK, BANK)
+            y_sb[c, m] = dst
+            nc.vector.scalar_tensor_tensor(out=dst, in0=e_ps[c, m], scalar=prior_sb[:, m : m + 1], in1=d_sb[half, m][:, lo : lo + CHUNK],
+                                           op0=ALU.add, op1=ALU.max)
 
-        def keep_larger(c, m):
-            gc, lo = divmod(c * CH, GW)
-            if m >= 4 - LATE and c + 1 < NCH and (c, m) != (NCH - 2, 3):
-                ys[c, m] = hb[c + 1][:].rearrange("p a n t -> p (a n t)").bitcast(F32)[:, (3 - m) * CH : (4 - m) * CH]
-            else:
-                ys[c, m] = take(ring_y)
-            nc.vector.scalar_tensor_tensor(out=ys[c, m][:], in0=es[c, m // 2][:, m % 2, :], scalar=pri[:, m : m + 1],
-                                           in1=dfs[gc, m][:, lo : lo + CH], op0=ALU.add, op1=ALU.max)
-
-        def put(c, m):
-            o = idx3[:, c * CH // 16 : (c + 1) * CH // 16]
-            nc.vector.tensor_tensor(out=page[m][:].indirect(o), in0=ys[c, m][:], in1=wg[:, c * CH : (c + 1) * CH], op=ALU.mult)
-            if c == NCH - 1:
+        def scatter(c, m):
+            nc.vector.tensor_tensor(out=page[m][:].indirect(entries(idx3, c * CHUNK, CHUNK)), in0=y_sb[c, m],
+                                    in1=wgo_sb[:, c * CHUNK : (c + 1) * CHUNK], op=ALU.mult)
+            if c == CHUNKS - 1:
                 nc.sync.dma_start(out=out[m * P : (m + 1) * P, :], in_=page[m][:])
 
-        units = [(a, jl) for a in range(2) for jl in range(JT)]
+        for half in range(HALVES):
+            nc.vector.tensor_copy(out=v_s[half][:], in_=tab_s[:].indirect(entries(idx, half * BANK, BANK)))
+        round_w1(0, nc.scalar.copy)
+        round_w1(1, nc.scalar.copy)
+        quantise_w1(0)
+        for c in range(CHUNKS):
+            half, lo = divmod(c * CHUNK, BANK)
+            nc.vector.tensor_copy(out=v_w[half][:, lo : lo + CHUNK], in_=tab_w[:].indirect(entries(idx, c * CHUNK, CHUNK)))
+        for jt in range(TILES):
+            make_a_and_sum(0, 0, jt)
+        round_w1(2, nc.vector.tensor_copy)
+        round_w1(3, nc.scalar.copy)
+        for jt in range(TILES):
+            make_a_and_sum(1, 0, jt)
+        quantise_w1(1)
+        for c in range(AHEAD):
+            for jt in range(TILES):
+                make_a_and_sum(c, 1, jt)
+        for g in range(PASSES):
+            nc.vector.tensor_copy(out=v2_w[g][:], in_=tab2_w[g][:].indirect(idx2[:]))
+        nc.vector.tensor_copy(out=v2_s[:], in_=tab2_s[:].indirect(idx2[:]))
 
-        gather_vs()
-        cast_w1(0, "s")
-        cast_w1(1, "s")
-        quant_w1(0)
-        gather_vw(0, CH)
-        gather_vw(CH, S)
-        for jl in range(JT):
-            first(0, 0, jl)
-            second(0, 0, jl)
-        cast_w1(2, "v")
-        cast_w1(3, "s")
-        for jl in range(JT):
-            first(1, 0, jl)
-            second(1, 0, jl)
-        quant_w1(1)
-        for c in range(2):
-            for jl in range(JT):
-                first(c, 1, jl)
-                second(c, 1, jl)
-        gather_v2w(0)
-        gather_v2w(1)
-        gather_v2s()
-        D_AT = {0: [(gc, m) for gc in range(2) for m in range(4)]}
-        for c in range(NCH):
-            for a in range(2):
-                for jl in range(JT):
-                    squash(c, a, jl)
-            for a in range(2):
-                finish(c, a)
-            quant_h(c)
-            if c + 1 == NCH:
-                break
-            late = [(c - 1, m) for m in range(4 - LATE, 4)] if c > 0 else []
-            for cm in late:
-                keep_larger(*cm)
-            if c + 2 < NCH:
-                for a, jl in units:
-                    first(c + 2, a, jl)
-                    second(c + 2, a, jl)
-            for gc, m in D_AT.get(c, []):
-                score_d(gc, m)
-            for pair in range(2):
-                score_e(c, pair)
-            for cm in late:
-                put(*cm)
-            for m in range(4 - LATE):
-                keep_larger(c, m)
-            for m in range(4 - LATE):
-                put(c, m)
-        steps = [(2, 2), (3, 2), (3, 0), (2, 3), (3, 3), (3, 1)]
-        for pair in (1, 0):
-            score_e(NCH - 1, pair)
-        keep_larger(*steps[0])
-        for i, cm in enumerate(steps):
+        last = CHUNKS - 1
+        for c in range(last):
+            make_h(c)
+            late = LATE if c > 0 else ()
+            for m in late:
+                make_y(c - 1, m, spent_h(c, m))
+            if c + AHEAD < CHUNKS:
+                for g in range(PASSES):
+                    for jt in range(TILES):
+                        make_a_and_sum(c + AHEAD, g, jt)
+            if c == 0:
+                for half in range(HALVES):
+                    for m in range(M_TILES):
+                        make_d(half, m)
+            make_e(c, EARLY)
+            make_e(c, LATE)
+            for m in late:
+                scatter(c - 1, m)
+            for m in EARLY:
+                make_y(c, m, take(y_ring))
+            for m in EARLY:
+                scatter(c, m)
+
+        make_h(last)
+        make_e(last, LATE)
+        make_e(last, EARLY)
+        steps = [step for m_late, m_early in zip(LATE, EARLY) for step in ((last - 1, m_late), (last, m_late), (last, m_early))]
+        make_y(*steps[0], spent_h(last, steps[0][1]))
+        for i, step in enumerate(steps):
             if i + 1 < len(steps):
-                keep_larger(*steps[i + 1])
-            put(*cm)
+                make_y(*steps[i + 1], take(y_ring))
+            scatter(*step)

from contextlib import ExitStack

import concourse.mybir as mybir
from concourse.masks import make_identity

K, T, S, H, T3, S2, T2 = 512, 2048, 1024, 1024, 2048, 512, 2048
FLOPS = 2 * S * (2 * K * H + H * S2 + K * S2)

F32 = mybir.dt.float32
BF16 = mybir.dt.bfloat16
I32 = mybir.dt.int32
U32 = mybir.dt.uint32
U16 = mybir.dt.uint16
U8 = mybir.dt.uint8
FP8X4 = mybir.dt.float8_e4m3fn_x4
FP4X4 = mybir.dt.float4_e2m1fn_x4
ALU = mybir.AluOpType
ACT = mybir.ActivationFunctionType

P = 128
PACK = 4
BANK = 512
PASSES = H // BANK
W1_PIECE = BANK // 2
CHUNK = 256
CHUNKS = S // CHUNK
TILES = CHUNK // P
HALVES = S // BANK
M_TILES = S2 // P
EARLY, LATE = (0, 1), (2, 3)
AHEAD = 2
GAIN_ON_VECTOR = (0, 1)


def tile_list_bridge_board_comparison_kernel(
    tc, tab_words, tab_scales, tab2_words, tab2_scales, w1, w4_words, w4_scales,
    w8_words, w8_scales, gain, prior, field, page1, wgo, offs, offs2, offs3, out,
):
    nc = tc.nc
    with ExitStack() as ctx:
        keep = ctx.enter_context(tc.tile_pool(name="keep", bufs=1))
        work = ctx.enter_context(tc.tile_pool(name="work", bufs=1))
        psum = ctx.enter_context(tc.psum_pool(name="psum", bufs=1))

        def held(shape, dtype, name):
            return keep.tile(shape, dtype, name=name, align_bytes=64)

        idx = held([P, S // 16], U16, "idx")
        idx2 = held([P, S2 // 16], U16, "idx2")
        idx3 = held([P, S // 16], U16, "idx3")
        tab_w = held([P, T], U32, "tab_w")
        tab_s = held([P, T], U8, "tab_s")
        tab2_w = [held([P, T3], U32, "tab2_w%d" % g) for g in range(PASSES)]
        tab2_s = held([P, T3], U8, "tab2_s")
        w1_raw = [held([P, PACK, W1_PIECE], F32, "w1_raw%d" % q) for q in range(H // W1_PIECE)]
        w1_bf = held([P, BANK, PACK], BF16, "w1_bf")
        w1_w = [held([P, BANK], U32, "w1_w%d" % g) for g in range(PASSES)]
        w1_s = [held([P, BANK], U8, "w1_s%d" % g) for g in range(PASSES)]
        w4_w = held([P, 2 * H], U8, "w4_w")
        w4_s = held([P, H], U8, "w4_s")
        w8_w = held([P, S2], U32, "w8_w")
        w8_s = held([P, S2], U8, "w8_s")
        gain_sb = held([P, PASSES, PACK], F32, "gain_sb")
        prior_sb = held([P, M_TILES], F32, "prior_sb")
        field_sb = [held([P, S], F32, "field_sb%d" % m) for m in range(M_TILES)]
        page = [held([P, T2], F32, "page%d" % m) for m in range(M_TILES)]
        wgo_sb = held([P, S], F32, "wgo_sb")
        ident = held([P, P], F32, "ident")
        v_w = [held([P, BANK], U32, "v_w%d" % half) for half in range(HALVES)]
        v_s = [held([P, BANK], U8, "v_s%d" % half) for half in range(HALVES)]
        v2_w = [held([P, S2], U32, "v2_w%d" % g) for g in range(PASSES)]
        v2_s = held([P, S2], U8, "v2_s")
        h_bf = [held([P, PASSES, CHUNK, PACK], BF16, "h_bf%d" % c) for c in range(CHUNKS)]
        h_w = [held([P, PASSES, CHUNK], U32, "h_w%d" % c) for c in range(CHUNKS)]
        h_s = [held([P, PASSES, CHUNK], U8, "h_s%d" % c) for c in range(CHUNKS)]

        for scale_tile in (tab_s, w4_s, tab2_s, w8_s):
            nc.vector.memset(scale_tile[:].bitcast(I32), 0)
        make_identity(nc, ident[:])

        def load_scales(scale_tile, dram, groups):
            rows = 4 * dram.shape[0]
            for q in groups:
                nc.sync.dma_start(out=scale_tile[32 * q : 32 * q + rows, :].bitcast(I32), in_=dram[:, 4 * q : 4 * q + 4, :].bitcast(I32))

        def load_words(tile, dram):
            nc.sync.dma_start(out=tile[:].bitcast(I32), in_=dram.rearrange("p t i -> p (t i)").bitcast(I32))

        def load_w1(q):
            by_partition = w1.rearrange("(p i) r -> p i r", i=PACK)
            nc.sync.dma_start(out=w1_raw[q][:], in_=by_partition[:, :, q * W1_PIECE : (q + 1) * W1_PIECE])

        def load_field(m):
            nc.sync.dma_start(out=field_sb[m][:], in_=field[m * P : (m + 1) * P, :])

        nc.sync.dma_start(idx[:], offs)
        load_scales(tab_s, tab_scales, range(4))
        nc.sync.dma_start(out=w4_w[:].bitcast(I32), in_=w4_words[0].bitcast(I32))
        load_w1(0)
        load_w1(1)
        load_scales(w4_s, w4_scales, range(4))
        load_words(tab_w, tab_words[0])
        load_w1(2)
        load_w1(3)
        nc.sync.dma_start(idx2[:], offs2)
        load_words(tab2_w[0], tab2_words[0])
        nc.sync.dma_start(out=gain_sb[:], in_=gain.rearrange("(g p t) -> p g t", g=PASSES, t=PACK))
        load_scales(tab2_s, tab2_scales, (0, 1))
        load_words(tab2_w[1], tab2_words[1])
        load_scales(tab2_s, tab2_scales, (2, 3))
        load_words(w8_w, w8_words[0])
        load_scales(w8_s, w8_scales, (0, 1))
        load_field(0)
        load_scales(w8_s, w8_scales, (2, 3))
        load_field(1)
        nc.sync.dma_start(idx3[:], offs3)
        load_field(2)
        with nc.allow_non_contiguous_dma(reason="four values of prior to a partition"):
            nc.sync.dma_start(out=prior_sb[:], in_=prior.rearrange("(m p) -> p m", p=P))
        load_field(3)
        nc.sync.dma_start(out=wgo_sb[:], in_=wgo)
        for m in range(M_TILES):
            nc.sync.dma_start(out=page[m][:], in_=page1[m * P : (m + 1) * P, :])

        def entries(index_tile, first, count):
            return index_tile[:, first // 16 : (first + count) // 16]

        def round_w1(q, copy):
            lo = q * W1_PIECE % BANK
            copy(out=w1_bf[:, lo : lo + W1_PIECE, :], in_=w1_raw[q][:].rearrange("p i r -> p r i"))

        def quantise_w1(g):
            nc.vector.quantize_mx(out=w1_w[g][:].bitcast(FP8X4), scales=w1_s[g][:], in_=w1_bf[:].rearrange("p r i -> p (r i)"))

        def deals(c, jt):
            half, lo = divmod(c * CHUNK + jt * P, BANK)
            return v_w[half][:, lo : lo + P].bitcast(FP8X4), v_s[half][:, lo : lo + P]

        def banks(name, count):
            return [psum.tile([P, BANK], F32, name="%s%d" % (name, i)) for i in range(count)]

        def take(ring):
            ring.append(ring.pop(0))
            return ring[-1][:]

        a_banks = banks("a_bank", 2)
        sum_banks = banks("sum_bank", 2)
        vector_banks = banks("vector_bank", 4)
        y_ring = [held([P, CHUNK], F32, "y%d" % i) for i in range(2)]
        per_chunk = PASSES * TILES
        a_sb, ab_sb, tanh_sb, d_sb, e_ps, y_sb = {}, {}, {}, {}, {}, {}

        def by_t(tile):
            return tile[:].rearrange("j (t p) -> j t p", t=PACK)

        def bank_by_t(bank):
            return bank.rearrange("j (p t) -> j t p", t=PACK)

        def make_a_and_sum(c, g, jt):
            words, scales = deals(c, jt)
            key = (c, g, jt)
            a_ps = take(a_banks)
            nc.tensor.matmul_mx(out=a_ps, lhsT=words, lhsT_scale=scales, rhs=w1_w[g][:].bitcast(FP8X4), rhs_scale=w1_s[g][:],
                                start=True, stop=True)
            a_sb[key] = work.tile([P, BANK], F32, name="a_sb", bufs=(AHEAD + 1) * per_chunk)
            nc.scalar.copy(out=by_t(a_sb[key]), in_=bank_by_t(a_ps))
            b_ps = take(vector_banks)
            nc.tensor.matmul_mx(out=b_ps, lhsT=words, lhsT_scale=scales,
                                rhs=w4_w[:, 2 * BANK * g : 2 * BANK * (g + 1)].bitcast(FP4X4),
                                rhs_scale=w4_s[:, BANK * g : BANK * (g + 1)], start=True, stop=True)
            ab_sb[key] = work.tile([P, BANK], F32, name="ab_sb", bufs=AHEAD * per_chunk)
            nc.vector.tensor_tensor(out=by_t(ab_sb[key]), in0=bank_by_t(b_ps), in1=by_t(a_sb[key]), op=ALU.add)

        def make_tanh(c, g, jt):
            tanh_sb[c, g, jt] = work.tile([P, BANK], F32, name="tanh_sb", bufs=per_chunk)
            nc.scalar.activation(out=tanh_sb[c, g, jt][:], in_=ab_sb[c, g, jt][:], func=ACT.Tanh)

        def turn_and_add(dst, c, g, jt, t):
            cols = slice(t * P, (t + 1) * P)
            nc.tensor.matmul(dst, lhsT=a_sb[c, g, jt][:, cols], rhs=ident[:], is_transpose=True, start=True, stop=False)
            nc.tensor.matmul(dst, lhsT=tanh_sb[c, g, jt][:, cols], rhs=ident[:], is_transpose=True, start=False, stop=True)

        def finish_h_on_scalar(c, g):
            h_by_t = work.tile([P, PACK, CHUNK], BF16, name="h_by_t", bufs=PASSES)
            per_bank = BANK // CHUNK
            for t0 in range(0, PACK, per_bank):
                sums = take(sum_banks).rearrange("p (t n) -> p t n", t=per_bank)
                for t in range(t0, t0 + per_bank):
                    for jt in range(TILES):
                        turn_and_add(sums[:, t - t0, jt * P : (jt + 1) * P], c, g, jt, t)
                for t in range(t0, t0 + per_bank):
                    nc.scalar.activation(out=h_by_t[:, t, :], in_=sums[:, t - t0, :], func=ACT.Copy, scale=gain_sb[:, g, t : t + 1])
            nc.scalar.copy(out=h_bf[c][:, g].rearrange("p (n i) t -> p n t i", i=4), in_=h_by_t[:].rearrange("p t (n i) -> p n t i", i=4))

        def finish_h_on_vector(c, g):
            for jt in range(TILES):
                sums = take(sum_banks).rearrange("p (t n) -> p t n", t=PACK)
                for t in range(PACK):
                    turn_and_add(sums[:, t, :], c, g, jt, t)
                nc.vector.tensor_tensor(out=h_bf[c][:, g, jt * P : (jt + 1) * P, :], in0=sums.rearrange("p t n -> p n t"),
                                        in1=gain_sb[:, g, :].unsqueeze(1).to_broadcast([P, P, PACK]), op=ALU.mult)

        def make_h(c):
            for g in range(PASSES):
                for jt in range(TILES):
                    make_tanh(c, g, jt)
            for g in range(PASSES):
                finish = finish_h_on_vector if (c, g) == GAIN_ON_VECTOR else finish_h_on_scalar
                finish(c, g)
            nc.vector.quantize_mx(out=h_w[c][:].rearrange("p g n -> p (g n)").bitcast(FP8X4), scales=h_s[c][:].rearrange("p g n -> p (g n)"),
                                  in_=h_bf[c][:].rearrange("p g n t -> p (g n t)"))

        def make_d(half, m):
            cols = slice(m * P, (m + 1) * P)
            d_ps = take(vector_banks)
            nc.tensor.matmul_mx(out=d_ps, lhsT=w8_w[:, cols].bitcast(FP8X4), lhsT_scale=w8_s[:, cols],
                                rhs=v_w[half][:].bitcast(FP8X4), rhs_scale=v_s[half][:], start=True, stop=True)
            d_sb[half, m] = work.tile([P, BANK], F32, name="d_sb", bufs=HALVES * M_TILES)
            nc.vector.tensor_tensor(out=d_sb[half, m][:], in0=d_ps, in1=field_sb[m][:, half * BANK : (half + 1) * BANK], op=ALU.add)

        def make_e(c, pair):
            bank = take(vector_banks).rearrange("p (i n) -> p i n", i=len(pair))
            for i, m in enumerate(pair):
                cols = slice(m * P, (m + 1) * P)
                for g in range(PASSES):
                    nc.tensor.matmul_mx(out=bank[:, i, :], lhsT=v2_w[g][:, cols].bitcast(FP8X4), lhsT_scale=v2_s[4 * g : P, cols],
                                        rhs=h_w[c][:, g, :].bitcast(FP8X4), rhs_scale=h_s[c][:, g, :],
                                        start=(g == 0), stop=(g == PASSES - 1))
                e_ps[c, m] = bank[:, i, :]

        def spent_h(c, m):
            slot = M_TILES - 1 - m
            return h_bf[c][:].rearrange("p g n t -> p (g n t)").bitcast(F32)[:, slot * CHUNK : (slot + 1) * CHUNK]

        def make_y(c, m, dst):
            half, lo = divmod(c * CHUNK, BANK)
            y_sb[c, m] = dst
            nc.vector.scalar_tensor_tensor(out=dst, in0=e_ps[c, m], scalar=prior_sb[:, m : m + 1], in1=d_sb[half, m][:, lo : lo + CHUNK],
                                           op0=ALU.add, op1=ALU.max)

        def scatter(c, m):
            nc.vector.tensor_tensor(out=page[m][:].indirect(entries(idx3, c * CHUNK, CHUNK)), in0=y_sb[c, m],
                                    in1=wgo_sb[:, c * CHUNK : (c + 1) * CHUNK], op=ALU.mult)
            if c == CHUNKS - 1:
                nc.sync.dma_start(out=out[m * P : (m + 1) * P, :], in_=page[m][:])

        for half in range(HALVES):
            nc.vector.tensor_copy(out=v_s[half][:], in_=tab_s[:].indirect(entries(idx, half * BANK, BANK)))
        round_w1(0, nc.scalar.copy)
        round_w1(1, nc.scalar.copy)
        quantise_w1(0)
        for c in range(CHUNKS):
            half, lo = divmod(c * CHUNK, BANK)
            nc.vector.tensor_copy(out=v_w[half][:, lo : lo + CHUNK], in_=tab_w[:].indirect(entries(idx, c * CHUNK, CHUNK)))
        for jt in range(TILES):
            make_a_and_sum(0, 0, jt)
        round_w1(2, nc.vector.tensor_copy)
        round_w1(3, nc.scalar.copy)
        for jt in range(TILES):
            make_a_and_sum(1, 0, jt)
        quantise_w1(1)
        for c in range(AHEAD):
            for jt in range(TILES):
                make_a_and_sum(c, 1, jt)
        for g in range(PASSES):
            nc.vector.tensor_copy(out=v2_w[g][:], in_=tab2_w[g][:].indirect(idx2[:]))
        nc.vector.tensor_copy(out=v2_s[:], in_=tab2_s[:].indirect(idx2[:]))

        last = CHUNKS - 1
        for c in range(last):
            make_h(c)
            late = LATE if c > 0 else ()
            for m in late:
                make_y(c - 1, m, spent_h(c, m))
            if c + AHEAD < CHUNKS:
                for g in range(PASSES):
                    for jt in range(TILES):
                        make_a_and_sum(c + AHEAD, g, jt)
            if c == 0:
                for half in range(HALVES):
                    for m in range(M_TILES):
                        make_d(half, m)
            make_e(c, EARLY)
            make_e(c, LATE)
            for m in late:
                scatter(c - 1, m)
            for m in EARLY:
                make_y(c, m, take(y_ring))
            for m in EARLY:
                scatter(c, m)

        make_h(last)
        make_e(last, LATE)
        make_e(last, EARLY)
        steps = [step for m_late, m_early in zip(LATE, EARLY) for step in ((last - 1, m_late), (last, m_late), (last, m_early))]
        make_y(*steps[0], spent_h(last, steps[0][1]))
        for i, step in enumerate(steps):
            if i + 1 < len(steps):
                make_y(*steps[i + 1], take(y_ring))
            scatter(*step)
